import numpy as np
import ml_dtypes


def mxq(x, axis, fmt="e4m3"):
    dtype, down = {"e4m3": (ml_dtypes.float8_e4m3fn, 7), "e5m2": (ml_dtypes.float8_e5m2, 14)}[fmt]
    v = np.moveaxis(np.asarray(x, np.float32).astype(ml_dtypes.bfloat16).astype(np.float64), axis, -1)
    blocks = v.reshape(v.shape[:-1] + (-1, 32))
    amax = np.abs(blocks).max(-1, keepdims=True)
    byte = np.maximum(np.where(amax > 0, np.frexp(amax)[1] - 1 + 127, 0) - down, 1)
    scale = np.exp2(byte - 127.0)
    codes = (blocks / scale).astype(np.float32).astype(dtype).astype(np.float64)
    return np.moveaxis((codes * scale).reshape(v.shape), -1, axis)


WIDE = False


def mx_kscale(k):
    if not WIDE:
        return np.ones(k)
    levels = np.array([10, -10, 5, -5, 0])
    if k % 512:
        return np.exp2(np.random.permutation(np.resize(levels, k // 32))).repeat(32)
    a = np.empty((k // 512, 16))
    for p in range(k // 512):
        a[p, :8] = np.random.permutation(np.resize(levels, 8))
        for g in range(8):
            far = levels[np.abs(levels - a[p, g]) >= 10]
            a[p, g + 8] = far[np.random.randint(len(far))]
    return np.exp2(a.ravel()).repeat(32)


def f64(x):
    return np.asarray(x).astype(np.float64)


def striped(idx):
    return np.tile(idx.reshape(-1, 16).T, (8, 1)).astype(np.uint16)


def unstriped(offs):
    return offs[:16].T.reshape(-1).astype(np.int64)


E2M1 = np.array([0.0, 0.5, 1.0, 1.5, 2.0, 3.0, 4.0, 6.0, -0.0, -0.5, -1.0, -1.5, -2.0, -3.0, -4.0, -6.0])


def pack_weight(w, fmt):
    k, n = w.shape
    w = f64(np.asarray(w, np.float32).astype(ml_dtypes.bfloat16)).reshape(k // 32, 32, n)
    amax = np.abs(w).max(1)
    if fmt == "e4m3":
        byte = np.frexp(amax)[1] - 1 + 127 - 7
    else:
        mant, ex = np.frexp(amax / 6.0)
        byte = np.where(mant > 0.5, ex, ex - 1) + 127
    byte = np.clip(np.where(amax > 0, byte, 1), 1, 254)
    scaled = (w * np.exp2(127.0 - byte)[:, None, :]).reshape(k, n).astype(np.float32)
    by_word = np.ascontiguousarray(scaled.reshape(k // 512, 128, 4, n).transpose(0, 1, 3, 2))
    if fmt == "e4m3":
        words = by_word.astype(ml_dtypes.float8_e4m3fn).view(np.uint8)
    else:
        c = by_word.astype(ml_dtypes.float4_e2m1fn).view(np.uint8) & 0xF
        words = (c[..., 0::2] | (c[..., 1::2] << 4)).reshape(k // 512, 128, 2 * n)
    return np.ascontiguousarray(words), np.ascontiguousarray(byte.astype(np.uint8).reshape(k // 512, 16, n))


def unpack_weight(words, scales, fmt):
    g, _, n = scales.shape
    words = np.ascontiguousarray(words).reshape(g, 128, n, -1)
    if fmt == "e4m3":
        vals = words.view(ml_dtypes.float8_e4m3fn).astype(np.float64)
    else:
        nib = np.empty((g, 128, n, 4), np.uint8)
        nib[..., 0::2] = words & 0xF
        nib[..., 1::2] = words >> 4
        vals = E2M1[nib]
    vals = vals * np.repeat(np.exp2(scales.astype(np.float64) - 127.0), 8, axis=1)[..., None]
    return vals.transpose(0, 1, 3, 2).reshape(g * 512, n)


def gelu(v):
    return 0.5 * v * (1.0 + np.tanh(np.sqrt(2.0 / np.pi) * (v + 0.044715 * v**3)))


def bf(x):
    return np.asarray(x, np.float32).astype(ml_dtypes.bfloat16)


def planes(Y):
    n, m = Y.shape
    b = f64(bf(Y)).reshape(n // 32, 32, m)
    amax = np.abs(b).max(1)
    byte = np.clip(np.where(amax > 0, np.frexp(amax)[1] - 1 + 127 - 7, 1), 1, 254)
    codes = (b * np.exp2(127.0 - byte)[:, None, :]).reshape(n, m).astype(np.float32).astype(ml_dtypes.float8_e4m3fn).view(np.uint8)
    words = codes.reshape(n // 512, 128, 4, m).transpose(0, 1, 3, 2)
    return np.ascontiguousarray(words), np.ascontiguousarray(byte.astype(np.uint8).reshape(n // 512, 16, m))


K, H, N, T, S, T2, P = 512, 1024, 512, 4096, 1024, 2048, 1024

def setup_inputs():
    n = np.random.standard_normal
    s = mx_kscale(K)[:, None]
    u = mx_kscale(H)[:, None]
    tab_words, tab_scales = pack_weight(n((K, T)) * s, "e4m3")
    w2_words, w2_scales = pack_weight(n((K, H)) / np.sqrt(K) / s, "e2m1")
    w3_words, w3_scales = pack_weight(n((K, H)) / np.sqrt(K) / s, "e4m3")
    return {
        "tab_words": tab_words, "tab_scales": tab_scales,
        "offs": striped(np.random.permutation(T)[:S]),
        "w1": (n((K, H)) / np.sqrt(K) / s).astype(np.float32),
        "w2_words": w2_words, "w2_scales": w2_scales,
        "w3_words": w3_words, "w3_scales": w3_scales,
        "wgs": np.exp(0.3 * n((128, S))).astype(np.float32),
        "offs2": striped(np.random.permutation(T2)[:S]),
        "offs3": striped(np.random.permutation(T2)[:P]),
        "gain": (np.exp(0.2 * n(H)) * u[:, 0]).astype(np.float32),
        "held": (0.7 * n((H, P)) * u).astype(np.float32),
        "wo": (n((H, N)) / np.sqrt(H) / u * np.exp(0.8 * n(N))).astype(np.float32),
    }

def reference(tab_words, tab_scales, offs, w1, w2_words, w2_scales, w3_words, w3_scales,
              wgs, offs2, offs3, gain, held, wo):
    v = unpack_weight(tab_words, tab_scales, "e4m3")[:, unstriped(offs)]
    a = mxq(f64(w1), 0, "e4m3").T @ v
    b = unpack_weight(w2_words, w2_scales, "e2m1").T @ v
    d = unpack_weight(w3_words, w3_scales, "e4m3").T @ v
    h = a + b * np.tanh(d)
    page = np.zeros((H, T2))
    page[:, unstriped(offs2)] = np.tile(f64(wgs), (H // 128, 1)) * h
    x = page[:, unstriped(offs3)]
    z = f64(gain)[:, None] * (x / (1 + np.exp(-x))) + f64(held)
    y = mxq(f64(wo), 0, "e4m3").T @ mxq(z, 0, "e4m3")
    words, scales = planes(y)
    return y, words, scales

@@ -1,0 +1,329 @@
+from contextlib import ExitStack
+
+import concourse.mybir as mybir
+from concourse.masks import make_identity
+
+K, H, N, T, S, T2, M = 512, 1024, 512, 4096, 1024, 2048, 1024
+FLOPS = 2 * (3 * K * H * S + H * N * M)
+
+F32 = mybir.dt.float32
+BF16 = mybir.dt.bfloat16
+I32 = mybir.dt.int32
+U32 = mybir.dt.uint32
+U16 = mybir.dt.uint16
+U8 = mybir.dt.uint8
+FP8X4 = mybir.dt.float8_e4m3fn_x4
+FP4X4 = mybir.dt.float4_e2m1fn_x4
+MULT = mybir.AluOpType.mult
+ADD = mybir.AluOpType.add
+ACT = mybir.ActivationFunctionType
+
+P = 128
+PACK = 4
+GROUP = P * PACK
+GROUPS = H // GROUP
+UNITS = S // P
+HALF = S // 2
+CHUNK = 256
+CHUNKS = M // CHUNK
+PER_COL = 16
+
+
+def tile_list_reshard_resume_features_kernel(
+    tc, tab_words, tab_scales, offs, w1, w2_words, w2_scales, w3_words, w3_scales,
+    wgs, offs2, offs3, gain, held, wo, out_0, out_1, out_2,
+):
+    nc = tc.nc
+    with ExitStack() as ctx:
+        keep = ctx.enter_context(tc.tile_pool(name="keep", bufs=1))
+        ring = ctx.enter_context(tc.tile_pool(name="ring", bufs=2))
+        psum = ctx.enter_context(tc.psum_pool(name="psum", bufs=1))
+
+        list1 = keep.tile([P, S // PER_COL], U16, name="list1")
+        list2 = keep.tile([P, S // PER_COL], U16, name="list2")
+        list3 = keep.tile([P, M // PER_COL], U16, name="list3")
+        tab_w = keep.tile([P, T], U32, name="tab_then_wg", align_bytes=64)
+        tab_s = keep.tile([P, T], U8, name="tab_s", align_bytes=64)
+        v_w = keep.tile([P, S], U32, name="v_w", align_bytes=64)
+        v_s = keep.tile([P, S], U8, name="v_s", align_bytes=64)
+        w1_w = keep.tile([P, H], U32, name="w1_w", align_bytes=64)
+        w1_s = keep.tile([P, H], U8, name="w1_s", align_bytes=64)
+        w2_w = keep.tile([P, 2 * H], U8, name="w2_w", align_bytes=64)
+        w2_s = keep.tile([P, H], U8, name="w2_s", align_bytes=64)
+        w3_w = keep.tile([P, H], U32, name="w3_w", align_bytes=64)
+        w3_s = keep.tile([P, H], U8, name="w3_s", align_bytes=64)
+        wo_w = keep.tile([P, GROUPS * N], U32, name="wo_w", align_bytes=64)
+        wo_s = keep.tile([P, GROUPS * N], U8, name="wo_s", align_bytes=64)
+        z_w = keep.tile([P, GROUPS * M], U32, name="z_w", align_bytes=64)
+        z_s = keep.tile([P, GROUPS * M], U8, name="z_s", align_bytes=64)
+        y_w = keep.tile([P, M], U32, name="y_w", align_bytes=64)
+        y_s = keep.tile([P, M], U8, name="y_s", align_bytes=64)
+        gain_sb = keep.tile([P, GROUPS, PACK], F32, name="gain_sb")
+        ident = keep.tile([P, P], F32, name="ident")
+        pages = [keep.tile([P, T2], F32, name=f"page{t}") for t in range(PACK)]
+
+        def load_scales(queue, plane, rows, quadrants):
+            for q in quadrants:
+                queue.dma_start(out=plane[32 * q : 32 * q + 4, :].bitcast(I32), in_=rows[0, 4 * q : 4 * q + 4, :].bitcast(I32))
+
+        def load_raw(rows):
+            raw = keep.tile([P, PACK, GROUP], F32, name="raw_then_held", align_bytes=64)
+            nc.sync.dma_start(out=raw[:], in_=rows.rearrange("(p i) c -> p i c", i=PACK))
+            return raw
+
+        def load_wgs(half):
+            cols = slice(half * HALF, (half + 1) * HALF)
+            for q in (0, 2, 1, 3):
+                nc.sync.dma_start(out=wg[32 * q : 32 * q + 32, :, cols], in_=wgs.rearrange("(p t) j -> p t j", t=PACK)[:, :, cols])
+
+        def load_held(g, tag):
+            rows = keep.tile([P, PACK, M], F32, name=tag, align_bytes=64)
+            nc.sync.dma_start(out=rows[:], in_=held[g * GROUP : (g + 1) * GROUP, :].rearrange("(p t) m -> p t m", t=PACK))
+            return rows
+
+        nc.sync.dma_start(list1[:], offs)
+        nc.sync.dma_start(list2[:], offs2)
+        nc.sync.dma_start(list3[:], offs3)
+        nc.sync.dma_start(out=tab_w[:].bitcast(I32), in_=tab_words[0].rearrange("p t i -> p (t i)").bitcast(I32))
+        w1_raw = {0: load_raw(w1[:, 0:GROUP])}
+        nc.sync.dma_start(out=w3_w[:].bitcast(I32), in_=w3_words[0].rearrange("p c i -> p (c i)").bitcast(I32))
+        nc.sync.dma_start(out=w2_w[:].bitcast(I32), in_=w2_words[0].bitcast(I32))
+        nc.vector.memset(tab_s[:].bitcast(I32), 0)
+        load_scales(nc.scalar, tab_s, tab_scales, range(4))
+        nc.gpsimd.memset(w3_s[:].bitcast(I32), 0)
+        load_scales(nc.gpsimd, w3_s, w3_scales, range(4))
+        nc.gpsimd.memset(w2_s[:].bitcast(I32), 0)
+        load_scales(nc.gpsimd, w2_s, w2_scales, range(2))
+        load_scales(nc.scalar, w2_s, w2_scales, range(2, 4))
+        make_identity(nc, ident[:])
+        for page in pages:
+            nc.vector.memset(page[:], 0.0)
+        nc.gpsimd.dma_start(out=gain_sb[:], in_=gain.rearrange("(g p t) -> p g t", p=P, t=PACK))
+
+        def gather_table(half):
+            cols = slice(half * HALF, (half + 1) * HALF)
+            entries = list1[:, half * HALF // PER_COL : (half + 1) * HALF // PER_COL]
+            nc.vector.tensor_copy(v_w[:, cols], tab_w[:].indirect(entries))
+            nc.vector.tensor_copy(v_s[:, cols], tab_s[:].indirect(entries))
+
+        def round_w1(g, copies):
+            staged = keep.tile([P, GROUP * PACK], BF16, name="staged_then_held", align_bytes=64)
+            width = GROUP // len(copies)
+            for c, copy in enumerate(copies):
+                copy(
+                    out=staged[:, c * width * PACK : (c + 1) * width * PACK].rearrange("p (c e i) -> p c i e", e=4, i=PACK),
+                    in_=w1_raw[g][:, :, c * width : (c + 1) * width].rearrange("p i (c e) -> p c i e", e=4),
+                )
+            return staged
+
+        def round_wo(raw):
+            staged = ring.tile([P, GROUP * PACK], BF16, name="staged", align_bytes=64)
+            nc.scalar.copy(
+                out=staged[:].rearrange("p (t c i) -> p c t i", t=PACK, i=PACK),
+                in_=raw.rearrange("p i (c t) -> p c t i", t=PACK),
+            )
+            return staged
+
+        def quantize(words, scales, g, staged):
+            cols = slice(g * GROUP, (g + 1) * GROUP)
+            nc.vector.quantize_mx(out=words[:, cols].bitcast(FP8X4), scales=scales[:, cols], in_=staged[:])
+
+        def dealt(bank):
+            return bank[:].rearrange("j (p t) -> j t p", t=PACK)
+
+        def product(bank, u, moving, moving_scales):
+            tokens = slice(u * P, (u + 1) * P)
+            nc.tensor.matmul_mx(
+                out=bank[:], lhsT=v_w[:, tokens].bitcast(FP8X4), lhsT_scale=v_s[:, tokens],
+                rhs=moving, rhs_scale=moving_scales, start=True, stop=True,
+            )
+
+        b_bank, tanh_d, a_sb, h_sb = {}, {}, {}, {}
+
+        def front_bd(g, u):
+            cols = slice(g * GROUP, (g + 1) * GROUP)
+            d_bank = psum.tile([P, GROUP], F32, name="ad_bank", bufs=2)
+            product(d_bank, u, w3_w[:, cols].bitcast(FP8X4), w3_s[:, cols])
+            b_bank[g, u] = psum.tile([P, GROUP], F32, name="b_bank", bufs=4)
+            product(b_bank[g, u], u, w2_w[:, 2 * g * GROUP : 2 * (g + 1) * GROUP].bitcast(FP4X4), w2_s[:, cols])
+            tanh_d[g, u] = ring.tile([P, PACK, P], F32, name="tanh_d", bufs=4)
+            nc.scalar.activation(out=tanh_d[g, u][:], in_=dealt(d_bank), func=ACT.Tanh)
+
+        def front_a(g, u, copy):
+            cols = slice(g * GROUP, (g + 1) * GROUP)
+            a_bank = psum.tile([P, GROUP], F32, name="ad_bank", bufs=2)
+            product(a_bank, u, w1_w[:, cols].bitcast(FP8X4), w1_s[:, cols])
+            a_sb[g, u] = ring.tile([P, PACK, P], F32, name="a_sb", bufs=4)
+            copy(out=a_sb[g, u][:], in_=dealt(a_bank))
+
+        def front(g, u):
+            front_bd(g, u)
+            front_a(g, u, nc.scalar.copy)
+
+        def back(g, u):
+            gated = ring.tile([P, PACK, P], F32, name="gated")
+            nc.vector.tensor_tensor(gated[:], dealt(b_bank[g, u]), tanh_d[g, u][:], MULT)
+            h_bank = psum.tile([P, PACK, P], F32, name="h_bank", bufs=2)
+            for t in range(PACK):
+                nc.tensor.matmul(h_bank[:, t, :], a_sb[g, u][:, t, :], ident[:], start=True, stop=False, is_transpose=True)
+                nc.tensor.matmul(h_bank[:, t, :], gated[:, t, :], ident[:], start=False, stop=True, is_transpose=True)
+            if u == 0:
+                h_sb[g] = ring.tile([P, PACK, S], F32, name="wide")
+            nc.scalar.copy(out=h_sb[g][:, :, u * P : (u + 1) * P], in_=h_bank[:])
+
+        def scatter(g, t, lo, hi):
+            entries = list2[:, lo // PER_COL : hi // PER_COL]
+            nc.vector.tensor_tensor(page_of(g, t)[:].indirect(entries), h_sb[g][:, t, lo:hi], wg[:, t, lo:hi], MULT)
+
+        held_sb, z_rows = {}, {}
+        x = keep.tile([P, M], F32, name="x")
+
+        def page_of(g, t):
+            return pages[t if g == 0 else 0]
+
+        def fetch(g, t, lo, hi):
+            nc.vector.tensor_copy(x[:, lo:hi], page_of(g, t)[:].indirect(list3[:, lo // PER_COL : hi // PER_COL]))
+            nc.scalar.activation(out=x[:, lo:hi], in_=x[:, lo:hi], func=ACT.Silu)
+
+        def make_z(g, t, lo, hi):
+            if t == 0:
+                z_rows[g] = keep.tile([P, PACK, M], BF16, name="z_rows")
+            nc.vector.scalar_tensor_tensor(
+                out=z_rows[g][:, t, lo:hi], in0=x[:, lo:hi], scalar=gain_sb[:, g, t : t + 1],
+                in1=held_sb[g][:, t, lo:hi], op0=MULT, op1=ADD,
+            )
+
+        z_woven = {}
+
+        def weave_z(copy, g, c):
+            z_woven[g, c] = ring.tile([P, CHUNK * PACK], BF16, name="z_woven", bufs=4, align_bytes=64)
+            copy(
+                out=z_woven[g, c][:].rearrange("p (c e t) -> p c t e", e=4, t=PACK),
+                in_=z_rows[g][:, :, c * CHUNK : (c + 1) * CHUNK].rearrange("p t (c e) -> p c t e", e=4),
+            )
+
+        def quantize_z(g, c):
+            cols = slice(g * M + c * CHUNK, g * M + (c + 1) * CHUNK)
+            nc.vector.quantize_mx(out=z_w[:, cols].bitcast(FP8X4), scales=z_s[:, cols], in_=z_woven[g, c][:])
+
+        y_bank = {}
+
+        def project(g, k):
+            if g == 0:
+                tag, bufs = ([("b_bank", 4)] * 4 + [("h_bank", 2)] * 2 + [("ad_bank", 2)] * 2)[k]
+                y_bank[k] = psum.tile([P, PACK, P], F32, name=tag, bufs=bufs)
+            cols = slice(g * M + k * P, g * M + (k + 1) * P)
+            for t in range(PACK):
+                rows = slice(g * N + t * P, g * N + (t + 1) * P)
+                nc.tensor.matmul_mx(
+                    out=y_bank[k][:, t, :], lhsT=wo_w[:, rows].bitcast(FP8X4), lhsT_scale=wo_s[:, rows],
+                    rhs=z_w[:, cols].bitcast(FP8X4), rhs_scale=z_s[:, cols],
+                    start=(g == 0 and t == 0), stop=(g == GROUPS - 1 and t == PACK - 1),
+                )
+
+        gather_table(0)
+        staged = round_w1(0, [nc.scalar.copy, nc.vector.tensor_copy])
+        for u in range(2):
+            front_bd(0, u)
+        quantize(w1_w, w1_s, 0, staged)
+        for u in range(2):
+            front_a(0, u, nc.vector.tensor_copy)
+        for u in range(2):
+            back(0, u)
+            front(0, 2 + u)
+        gather_table(1)
+        wg = keep.tile([P, PACK, S], F32, name="tab_then_wg", align_bytes=64)
+        load_wgs(0)
+        w1_raw[1] = load_raw(w1[:, GROUP : 2 * GROUP])
+        load_wgs(1)
+        for u in range(2, 4):
+            back(0, u)
+        for u in range(4, UNITS):
+            front(0, u)
+        staged = round_w1(1, [nc.scalar.copy] * 4)
+        held_sb[0] = load_held(0, "raw_then_held")
+        quantize(w1_w, w1_s, 1, staged)
+        held_sb[1] = load_held(1, "staged_then_held")
+        later = [(0, u) for u in range(4, UNITS)] + [(1, u) for u in range(UNITS)]
+
+        def advance():
+            g, u = later.pop(0)
+            back(g, u)
+            if len(later) >= 4:
+                front(*later[3])
+
+        for quarter in range(3):
+            for t in range(PACK):
+                scatter(0, t, quarter * CHUNK, (quarter + 1) * CHUNK)
+                if t % 2 == 0:
+                    advance()
+        for t in range(PACK):
+            scatter(0, t, 3 * CHUNK, S)
+            if t > 0:
+                make_z(0, t - 1, 0, M)
+            fetch(0, t, 0, M)
+            while len(later) > 2 * max(2 - t, 0):
+                advance()
+        wo_raw = ring.tile([P, GROUPS, PACK, N], F32, name="wide")
+        for g in range(GROUPS):
+            nc.sync.dma_start(out=wo_raw[:, g], in_=wo[g * GROUP : (g + 1) * GROUP, :].rearrange("(p i) n -> p i n", i=PACK))
+        for t in range(PACK):
+            if t == 0:
+                scatter(1, t, 0, HALF)
+                scatter(1, t, HALF, S)
+            else:
+                scatter(1, t, 0, S)
+            if t == 0:
+                make_z(0, 3, 0, M)
+                for c in range(CHUNKS):
+                    weave_z(nc.scalar.copy, 0, c)
+                wo_staged = [round_wo(wo_raw[:, g]) for g in range(GROUPS)]
+            else:
+                make_z(1, t - 1, 0, M)
+                if t == 1:
+                    for c in range(CHUNKS):
+                        quantize_z(0, c)
+                if t == 2:
+                    for g in range(GROUPS):
+                        quantize(wo_w, wo_s, g, wo_staged[g])
+                    for k in range(M // P):
+                        project(0, k)
+            if t < PACK - 1:
+                fetch(1, t, 0, M)
+
+        y_sb = ring.tile([P, PACK, M], F32, name="wide")
+        y_woven = {}
+        last = PACK - 1
+
+        def empty_y(c):
+            y_woven[c] = ring.tile([P, CHUNK * PACK], BF16, name="y_woven", align_bytes=64)
+            for e in range(CHUNK // P):
+                k = c * (CHUNK // P) + e
+                project(1, k)
+                (nc.scalar.copy if c < CHUNKS // 2 else nc.vector.tensor_copy)(
+                    out=y_woven[c][:, e * GROUP : (e + 1) * GROUP].rearrange("p (m t) -> p m t", t=PACK),
+                    in_=y_bank[k][:].rearrange("p t m -> p m t"),
+                )
+                nc.scalar.copy(out=y_sb[:, :, k * P : (k + 1) * P], in_=y_bank[k][:])
+            cols = slice(c * CHUNK, (c + 1) * CHUNK)
+            nc.sync.dma_start(out=out_0.rearrange("(p t) m -> p t m", t=PACK)[:, :, cols], in_=y_sb[:, :, cols])
+
+        def quantize_y(c):
+            cols = slice(c * CHUNK, (c + 1) * CHUNK)
+            nc.vector.quantize_mx(out=y_w[:, cols].bitcast(FP8X4), scales=y_s[:, cols], in_=y_woven[c][:])
+            nc.sync.dma_start(out=out_1[0].rearrange("p m t -> p (m t)").bitcast(I32)[:, cols], in_=y_w[:, cols].bitcast(I32))
+
+        stages = [
+            lambda c: fetch(1, last, c * CHUNK, (c + 1) * CHUNK),
+            lambda c: make_z(1, last, c * CHUNK, (c + 1) * CHUNK),
+            lambda c: weave_z(nc.vector.tensor_copy, 1, c),
+            lambda c: quantize_z(1, c),
+            empty_y,
+            quantize_y,
+        ]
+        for step in range(CHUNKS + len(stages) - 1):
+            for depth, stage in enumerate(stages):
+                if 0 <= step - depth < CHUNKS:
+                    stage(step - depth)
+        for q in range(4):
+            nc.sync.dma_start(out=out_2[0, 4 * q : 4 * q + 4, :].bitcast(I32), in_=y_s[32 * q : 32 * q + 4, :].bitcast(I32))

@@ -173,30 +173,31 @@ def tile_list_reshard_resume_features_kernel(
 
         def scatter(g, t, lo, hi):
             entries = list2[:, lo // PER_COL : hi // PER_COL]
-            nc.vector.tensor_tensor(page_of(g, t)[:].indirect(entries), h_sb[g][:, t, lo:hi], wg[:, t, lo:hi], MULT)
+            nc.gpsimd.tensor_tensor(h_sb[g][:, t, lo:hi], h_sb[g][:, t, lo:hi], wg[:, t, lo:hi], MULT)
+            nc.vector.tensor_copy(page_of(g, t)[:].indirect(entries), h_sb[g][:, t, lo:hi])
 
         held_sb, z_rows = {}, {}
-        x = keep.tile([P, M], F32, name="x")
+        xs = [keep.tile([P, M], F32, name=f"x{e}") for e in range(2)]
 
         def page_of(g, t):
             return pages[t if g == 0 else 0]
 
         def fetch(g, t, lo, hi):
+            x = xs[t % 2]
             nc.vector.tensor_copy(x[:, lo:hi], page_of(g, t)[:].indirect(list3[:, lo // PER_COL : hi // PER_COL]))
             nc.scalar.activation(out=x[:, lo:hi], in_=x[:, lo:hi], func=ACT.Silu)
 
         def make_z(g, t, lo, hi):
+            x = xs[t % 2]
             if t == 0:
                 z_rows[g] = keep.tile([P, PACK, M], BF16, name="z_rows")
-            nc.vector.scalar_tensor_tensor(
-                out=z_rows[g][:, t, lo:hi], in0=x[:, lo:hi], scalar=gain_sb[:, g, t : t + 1],
-                in1=held_sb[g][:, t, lo:hi], op0=MULT, op1=ADD,
-            )
+            nc.scalar.activation(out=x[:, lo:hi], in_=x[:, lo:hi], func=ACT.Copy, scale=gain_sb[:, g, t : t + 1])
+            nc.gpsimd.tensor_tensor(z_rows[g][:, t, lo:hi], x[:, lo:hi], held_sb[g][:, t, lo:hi], ADD)
 
         z_woven = {}
 
         def weave_z(copy, g, c):
-            z_woven[g, c] = ring.tile([P, CHUNK * PACK], BF16, name="z_woven", bufs=4, align_bytes=64)
+            z_woven[g, c] = keep.tile([P, CHUNK * PACK], BF16, name=f"z_woven{c}", align_bytes=64)
             copy(
                 out=z_woven[g, c][:].rearrange("p (c e t) -> p c t e", e=4, t=PACK),
                 in_=z_rows[g][:, :, c * CHUNK : (c + 1) * CHUNK].rearrange("p t (c e) -> p c t e", e=4),
@@ -294,36 +295,55 @@ def tile_list_reshard_resume_features_kernel(
         y_sb = ring.tile([P, PACK, M], F32, name="wide")
         y_woven = {}
         last = PACK - 1
+        x_last = {}
 
         def empty_y(c):
             y_woven[c] = ring.tile([P, CHUNK * PACK], BF16, name="y_woven", align_bytes=64)
             for e in range(CHUNK // P):
                 k = c * (CHUNK // P) + e
                 project(1, k)
-                (nc.scalar.copy if c < CHUNKS // 2 else nc.vector.tensor_copy)(
-                    out=y_woven[c][:, e * GROUP : (e + 1) * GROUP].rearrange("p (m t) -> p m t", t=PACK),
-                    in_=y_bank[k][:].rearrange("p t m -> p m t"),
-                )
                 nc.scalar.copy(out=y_sb[:, :, k * P : (k + 1) * P], in_=y_bank[k][:])
             cols = slice(c * CHUNK, (c + 1) * CHUNK)
             nc.sync.dma_start(out=out_0.rearrange("(p t) m -> p t m", t=PACK)[:, :, cols], in_=y_sb[:, :, cols])
+
+        def weave_y(c):
+            nc.vector.tensor_copy(
+                out=y_woven[c][:].rearrange("p (m e t) -> p m t e", e=4, t=PACK),
+                in_=y_sb[:, :, c * CHUNK : (c + 1) * CHUNK].rearrange("p t (m e) -> p m t e", e=4),
+            )
 
         def quantize_y(c):
             cols = slice(c * CHUNK, (c + 1) * CHUNK)
             nc.vector.quantize_mx(out=y_w[:, cols].bitcast(FP8X4), scales=y_s[:, cols], in_=y_woven[c][:])
             nc.sync.dma_start(out=out_1[0].rearrange("p m t -> p (m t)").bitcast(I32)[:, cols], in_=y_w[:, cols].bitcast(I32))
 
-        stages = [
-            lambda c: fetch(1, last, c * CHUNK, (c + 1) * CHUNK),
-            lambda c: make_z(1, last, c * CHUNK, (c + 1) * CHUNK),
-            lambda c: weave_z(nc.vector.tensor_copy, 1, c),
-            lambda c: quantize_z(1, c),
-            empty_y,
-            quantize_y,
-        ]
-        for step in range(CHUNKS + len(stages) - 1):
-            for depth, stage in enumerate(stages):
-                if 0 <= step - depth < CHUNKS:
-                    stage(step - depth)
+        def fetch_last(c):
+            if c < 2:
+                x = xs[last % 2][:, c * CHUNK : (c + 1) * CHUNK]
+            else:
+                x = keep.tile([P, CHUNK], F32, name=f"z_woven{c - 2}", align_bytes=64)[:]
+            x_last[c] = x
+            nc.vector.tensor_copy(x, page_of(1, last)[:].indirect(list3[:, c * CHUNK // PER_COL : (c + 1) * CHUNK // PER_COL]))
+            nc.scalar.activation(out=x, in_=x, func=ACT.Silu)
+
+        def make_last(c):
+            cols = slice(c * CHUNK, (c + 1) * CHUNK)
+            nc.vector.scalar_tensor_tensor(
+                out=z_rows[1][:, last, cols], in0=x_last[c],
+                scalar=gain_sb[:, 1, last : last + 1], in1=held_sb[1][:, last, cols], op0=MULT, op1=ADD,
+            )
+
+        fetch_last(0)
+        fetch_last(1)
+        for c in range(CHUNKS):
+            make_last(c)
+            weave_z(nc.scalar.copy if c == 1 else nc.vector.tensor_copy, 1, c)
+            quantize_z(1, c)
+            if c + 2 < CHUNKS:
+                fetch_last(c + 2)
+        for c in range(CHUNKS):
+            empty_y(c)
+            weave_y(c)
+            quantize_y(c)
         for q in range(4):
             nc.sync.dma_start(out=out_2[0, 4 * q : 4 * q + 4, :].bitcast(I32), in_=y_s[32 * q : 32 * q + 4, :].bitcast(I32))

@@ -26,7 +26,11 @@ UNITS = S // P
 HALF = S // 2
 CHUNK = 256
 CHUNKS = M // CHUNK
+QUARTERS = S // CHUNK
 PER_COL = 16
+ZS = (0, 1)
+YS = (0, 1)
+LAG = 1
 
 
 def tile_list_reshard_resume_features_kernel(
@@ -43,10 +47,9 @@ def tile_list_reshard_resume_features_kernel(
         list2 = keep.tile([P, S // PER_COL], U16, name="list2")
         list3 = keep.tile([P, M // PER_COL], U16, name="list3")
         tab_w = keep.tile([P, T], U32, name="tab_then_wg", align_bytes=64)
-        tab_s = keep.tile([P, T], U8, name="tab_s", align_bytes=64)
+        tab_s = keep.tile([P, T], U8, name="tab_s_then_w1", align_bytes=64)
         v_w = keep.tile([P, S], U32, name="v_w", align_bytes=64)
         v_s = keep.tile([P, S], U8, name="v_s", align_bytes=64)
-        w1_w = keep.tile([P, H], U32, name="w1_w", align_bytes=64)
         w1_s = keep.tile([P, H], U8, name="w1_s", align_bytes=64)
         w2_w = keep.tile([P, 2 * H], U8, name="w2_w", align_bytes=64)
         w2_s = keep.tile([P, H], U8, name="w2_s", align_bytes=64)
@@ -66,15 +69,13 @@ def tile_list_reshard_resume_features_kernel(
             for q in quadrants:
                 queue.dma_start(out=plane[32 * q : 32 * q + 4, :].bitcast(I32), in_=rows[0, 4 * q : 4 * q + 4, :].bitcast(I32))
 
-        def load_raw(rows):
-            raw = keep.tile([P, PACK, GROUP], F32, name="raw_then_held", align_bytes=64)
-            nc.sync.dma_start(out=raw[:], in_=rows.rearrange("(p i) c -> p i c", i=PACK))
+        def load_raw(raw, rows):
+            nc.sync.dma_start(out=raw, in_=rows.rearrange("(p i) c -> p i c", i=PACK))
             return raw
 
-        def load_wgs(half):
-            cols = slice(half * HALF, (half + 1) * HALF)
+        def load_wgs(part, lo, hi):
             for q in (0, 2, 1, 3):
-                nc.sync.dma_start(out=wg[32 * q : 32 * q + 32, :, cols], in_=wgs.rearrange("(p t) j -> p t j", t=PACK)[:, :, cols])
+                nc.sync.dma_start(out=part[32 * q : 32 * q + 32], in_=wgs.rearrange("(p t) j -> p t j", t=PACK)[:, :, lo:hi])
 
         def load_held(g, tag):
             rows = keep.tile([P, PACK, M], F32, name=tag, align_bytes=64)
@@ -85,19 +86,23 @@ def tile_list_reshard_resume_features_kernel(
         nc.sync.dma_start(list2[:], offs2)
         nc.sync.dma_start(list3[:], offs3)
         nc.sync.dma_start(out=tab_w[:].bitcast(I32), in_=tab_words[0].rearrange("p t i -> p (t i)").bitcast(I32))
-        w1_raw = {0: load_raw(w1[:, 0:GROUP])}
+        raw_first = keep.tile([P, PACK, GROUP], F32, name="raw_then_wg")
+        load_raw(raw_first[:], w1[:, 0:GROUP])
         nc.sync.dma_start(out=w3_w[:].bitcast(I32), in_=w3_words[0].rearrange("p c i -> p (c i)").bitcast(I32))
         nc.sync.dma_start(out=w2_w[:].bitcast(I32), in_=w2_words[0].bitcast(I32))
         nc.vector.memset(tab_s[:].bitcast(I32), 0)
         load_scales(nc.scalar, tab_s, tab_scales, range(4))
         nc.gpsimd.memset(w3_s[:].bitcast(I32), 0)
         load_scales(nc.gpsimd, w3_s, w3_scales, range(4))
-        nc.gpsimd.memset(w2_s[:].bitcast(I32), 0)
-        load_scales(nc.gpsimd, w2_s, w2_scales, range(2))
-        load_scales(nc.scalar, w2_s, w2_scales, range(2, 4))
+        nc.vector.memset(w2_s[:].bitcast(I32), 0)
+        load_scales(nc.gpsimd, w2_s, w2_scales, range(3))
+        load_scales(nc.scalar, w2_s, w2_scales, range(3, 4))
         make_identity(nc, ident[:])
-        for page in pages:
-            nc.vector.memset(page[:], 0.0)
+        for page in pages[:2]:
+            nc.vector.memset(page[:, : T2 // 2 - 1], 0.0)
+            nc.vector.memset(page[:, T2 // 2 - 1 :], 0.0)
+        for page in pages[2:]:
+            nc.gpsimd.memset(page[:], 0.0)
         nc.gpsimd.dma_start(out=gain_sb[:], in_=gain.rearrange("(g p t) -> p g t", p=P, t=PACK))
 
         def gather_table(half):
@@ -106,22 +111,24 @@ def tile_list_reshard_resume_features_kernel(
             nc.vector.tensor_copy(v_w[:, cols], tab_w[:].indirect(entries))
             nc.vector.tensor_copy(v_s[:, cols], tab_s[:].indirect(entries))
 
-        def round_w1(g, copies):
-            staged = keep.tile([P, GROUP * PACK], BF16, name="staged_then_held", align_bytes=64)
-            width = GROUP // len(copies)
-            for c, copy in enumerate(copies):
-                copy(
+        def round_w1(g, raw, pieces):
+            staged = keep.tile([P, GROUP * PACK], BF16, name=f"staged_then_held{g}", align_bytes=64)
+            width = GROUP // pieces
+            for c in range(pieces):
+                nc.scalar.copy(
                     out=staged[:, c * width * PACK : (c + 1) * width * PACK].rearrange("p (c e i) -> p c i e", e=4, i=PACK),
-                    in_=w1_raw[g][:, :, c * width : (c + 1) * width].rearrange("p i (c e) -> p c i e", e=4),
+                    in_=raw[:, :, c * width : (c + 1) * width].rearrange("p i (c e) -> p c i e", e=4),
                 )
             return staged
 
-        def round_wo(raw):
-            staged = ring.tile([P, GROUP * PACK], BF16, name="staged", align_bytes=64)
-            nc.scalar.copy(
-                out=staged[:].rearrange("p (t c i) -> p c t i", t=PACK, i=PACK),
-                in_=raw.rearrange("p i (c t) -> p c t i", t=PACK),
-            )
+        def round_wo(g, raw):
+            staged = keep.tile([P, GROUP * PACK], BF16, name=f"staged_then_held{g}", align_bytes=64)
+            width = P // 4
+            for c in range(4):
+                nc.scalar.copy(
+                    out=staged[:].rearrange("p (t c i) -> p c t i", t=PACK, i=PACK)[:, c * width : (c + 1) * width],
+                    in_=raw.rearrange("p i (c t) -> p c t i", t=PACK)[:, c * width : (c + 1) * width],
+                )
             return staged
 
         def quantize(words, scales, g, staged):
@@ -142,65 +149,81 @@ def tile_list_reshard_resume_features_kernel(
 
         def front_bd(g, u):
             cols = slice(g * GROUP, (g + 1) * GROUP)
-            d_bank = psum.tile([P, GROUP], F32, name="ad_bank", bufs=2)
+            if u % 2 == 1:
+                d_bank = psum.tile([P, GROUP], F32, name="chain_bank")
+            else:
+                d_bank = psum.tile([P, GROUP], F32, name="ad_bank", bufs=2)
             product(d_bank, u, w3_w[:, cols].bitcast(FP8X4), w3_s[:, cols])
-            b_bank[g, u] = psum.tile([P, GROUP], F32, name="b_bank", bufs=4)
+            b_bank[g, u] = psum.tile([P, GROUP], F32, name="b_bank", bufs=2)
             product(b_bank[g, u], u, w2_w[:, 2 * g * GROUP : 2 * (g + 1) * GROUP].bitcast(FP4X4), w2_s[:, cols])
-            tanh_d[g, u] = ring.tile([P, PACK, P], F32, name="tanh_d", bufs=4)
+            tanh_d[g, u] = ring.tile([P, PACK, P], F32, name="tanh_d", bufs=2)
             nc.scalar.activation(out=tanh_d[g, u][:], in_=dealt(d_bank), func=ACT.Tanh)
 
-        def front_a(g, u, copy):
+        def front_a(g, u):
             cols = slice(g * GROUP, (g + 1) * GROUP)
             a_bank = psum.tile([P, GROUP], F32, name="ad_bank", bufs=2)
             product(a_bank, u, w1_w[:, cols].bitcast(FP8X4), w1_s[:, cols])
             a_sb[g, u] = ring.tile([P, PACK, P], F32, name="a_sb", bufs=4)
-            copy(out=a_sb[g, u][:], in_=dealt(a_bank))
+            nc.scalar.copy(out=a_sb[g, u][:], in_=dealt(a_bank))
 
-        def front(g, u):
-            front_bd(g, u)
-            front_a(g, u, nc.scalar.copy)
+        gated = {}
 
-        def back(g, u):
-            gated = ring.tile([P, PACK, P], F32, name="gated")
-            nc.vector.tensor_tensor(gated[:], dealt(b_bank[g, u]), tanh_d[g, u][:], MULT)
-            h_bank = psum.tile([P, PACK, P], F32, name="h_bank", bufs=2)
-            for t in range(PACK):
-                nc.tensor.matmul(h_bank[:, t, :], a_sb[g, u][:, t, :], ident[:], start=True, stop=False, is_transpose=True)
-                nc.tensor.matmul(h_bank[:, t, :], gated[:, t, :], ident[:], start=False, stop=True, is_transpose=True)
-            if u == 0:
+        def gate(g, u):
+            gated[g, u] = ring.tile([P, PACK, P], F32, name="gated", bufs=4)
+            nc.vector.tensor_tensor(gated[g, u][:], dealt(b_bank[g, u]), tanh_d[g, u][:], MULT)
+
+        def back(g, quarter, pair):
+            if (quarter, pair) == (0, 0):
                 h_sb[g] = ring.tile([P, PACK, S], F32, name="wide")
-            nc.scalar.copy(out=h_sb[g][:, :, u * P : (u + 1) * P], in_=h_bank[:])
+            if pair == 0:
+                h_bank = psum.tile([P, 2, CHUNK], F32, name="turn_bank", bufs=3)
+            else:
+                h_bank = psum.tile([P, 2, CHUNK], F32, name="chain_bank")
+            if True:
+                for e in range(2):
+                    for uu in range(2):
+                        u, t = 2 * quarter + uu, 2 * pair + e
+                        out = h_bank[:, e, uu * P : (uu + 1) * P]
+                        nc.tensor.matmul(out, a_sb[g, u][:, t, :], ident[:], start=True, stop=False, is_transpose=True)
+                        nc.tensor.matmul(out, gated[g, u][:, t, :], ident[:], start=False, stop=True, is_transpose=True)
+                nc.scalar.copy(out=h_sb[g][:, 2 * pair : 2 * pair + 2, quarter * CHUNK : (quarter + 1) * CHUNK], in_=h_bank[:])
 
         def scatter(g, t, lo, hi):
             entries = list2[:, lo // PER_COL : hi // PER_COL]
-            nc.gpsimd.tensor_tensor(h_sb[g][:, t, lo:hi], h_sb[g][:, t, lo:hi], wg[:, t, lo:hi], MULT)
-            nc.vector.tensor_copy(page_of(g, t)[:].indirect(entries), h_sb[g][:, t, lo:hi])
+            nc.vector.tensor_tensor(pages[t][:].indirect(entries), h_sb[g][:, t, lo:hi], wg[lo // HALF][:, t, lo % HALF : lo % HALF + hi - lo], MULT)
 
-        held_sb, z_rows = {}, {}
-        xs = [keep.tile([P, M], F32, name=f"x{e}") for e in range(2)]
+        held_sb, z_woven = {}, {}
 
-        def page_of(g, t):
-            return pages[t if g == 0 else 0]
+        def new_woven(g, c):
+            z_woven[g, c] = ring.tile([P, CHUNK * PACK], BF16, name="z_woven", bufs=CHUNKS, align_bytes=64)
+            return z_woven[g, c]
 
-        def fetch(g, t, lo, hi):
-            x = xs[t % 2]
-            nc.vector.tensor_copy(x[:, lo:hi], page_of(g, t)[:].indirect(list3[:, lo // PER_COL : hi // PER_COL]))
-            nc.scalar.activation(out=x[:, lo:hi], in_=x[:, lo:hi], func=ACT.Silu)
+        def fetch_rows(t):
+            x = keep.tile([P, M], F32, name=f"x{t}")
+            nc.vector.tensor_copy(x[:], pages[t][:].indirect(list3[:]))
+            nc.scalar.activation(out=x[:], in_=x[:], func=ACT.Silu)
+            return x
 
-        def make_z(g, t, lo, hi):
-            x = xs[t % 2]
-            if t == 0:
-                z_rows[g] = keep.tile([P, PACK, M], BF16, name="z_rows")
-            nc.scalar.activation(out=x[:, lo:hi], in_=x[:, lo:hi], func=ACT.Copy, scale=gain_sb[:, g, t : t + 1])
-            nc.gpsimd.tensor_tensor(z_rows[g][:, t, lo:hi], x[:, lo:hi], held_sb[g][:, t, lo:hi], ADD)
+        def add_held_turned(pair, rows):
+            turned = keep.tile([P, M // P, P, 2], BF16, name=f"turned{pair}")
+            for c in range(CHUNKS):
+                bank = psum.tile([P, 2, 2, P], F32, name="turn_bank", bufs=3)
+                for kk in range(2):
+                    cols = slice(c * CHUNK + kk * P, c * CHUNK + (kk + 1) * P)
+                    for e in range(2):
+                        nc.tensor.matmul(bank[:, kk, e, :], rows[e][:, cols], ident[:], start=True, stop=False, is_transpose=True)
+                        nc.tensor.matmul(bank[:, kk, e, :], held_sb[0][:, 2 * pair + e, cols], ident[:], start=False, stop=True, is_transpose=True)
+                nc.scalar.copy(out=turned[:, 2 * c : 2 * c + 2], in_=bank[:].rearrange("m k e p -> m k p e"))
+            return turned[:].rearrange("m k p e -> m (k p e)").bitcast(F32)
 
-        z_woven = {}
-
-        def weave_z(copy, g, c):
-            z_woven[g, c] = keep.tile([P, CHUNK * PACK], BF16, name=f"z_woven{c}", align_bytes=64)
-            copy(
-                out=z_woven[g, c][:].rearrange("p (c e t) -> p c t e", e=4, t=PACK),
-                in_=z_rows[g][:, :, c * CHUNK : (c + 1) * CHUNK].rearrange("p t (c e) -> p c t e", e=4),
+        def turn_back(pairs, c):
+            bank = psum.tile([P, 2, CHUNK], F32, name="turn_bank", bufs=3)
+            for pair in range(2):
+                for kk in range(2):
+                    k = 2 * c + kk
+                    nc.tensor.transpose(bank[:, pair, kk * P : (kk + 1) * P], pairs[pair][:, k * P : (k + 1) * P], ident[:])
+            nc.scalar.copy(
+                out=new_woven(0, c)[:].bitcast(F32).rearrange("p (m u) -> p m u", u=2), in_=bank[:].rearrange("p u m -> p m u")
             )
 
         def quantize_z(g, c):
@@ -211,7 +234,7 @@ def tile_list_reshard_resume_features_kernel(
 
         def project(g, k):
             if g == 0:
-                tag, bufs = ([("b_bank", 4)] * 4 + [("h_bank", 2)] * 2 + [("ad_bank", 2)] * 2)[k]
+                tag, bufs = ([("b_bank", 2)] * 2 + [("ad_bank", 2)] * 2 + [("chain_bank", 1)] + [("turn_bank", 3)] * 3)[k]
                 y_bank[k] = psum.tile([P, PACK, P], F32, name=tag, bufs=bufs)
             cols = slice(g * M + k * P, g * M + (k + 1) * P)
             for t in range(PACK):
@@ -223,82 +246,66 @@ def tile_list_reshard_resume_features_kernel(
                 )
 
         gather_table(0)
-        staged = round_w1(0, [nc.scalar.copy, nc.vector.tensor_copy])
+        gather_table(1)
+        staged = round_w1(0, raw_first[:], 1)
         for u in range(2):
             front_bd(0, u)
+        w1_w = keep.tile([P, H], U32, name="tab_s_then_w1", align_bytes=64)
         quantize(w1_w, w1_s, 0, staged)
         for u in range(2):
-            front_a(0, u, nc.vector.tensor_copy)
-        for u in range(2):
-            back(0, u)
-            front(0, 2 + u)
-        gather_table(1)
-        wg = keep.tile([P, PACK, S], F32, name="tab_then_wg", align_bytes=64)
-        load_wgs(0)
-        w1_raw[1] = load_raw(w1[:, GROUP : 2 * GROUP])
-        load_wgs(1)
-        for u in range(2, 4):
-            back(0, u)
-        for u in range(4, UNITS):
-            front(0, u)
-        staged = round_w1(1, [nc.scalar.copy] * 4)
-        held_sb[0] = load_held(0, "raw_then_held")
-        quantize(w1_w, w1_s, 1, staged)
-        held_sb[1] = load_held(1, "staged_then_held")
-        later = [(0, u) for u in range(4, UNITS)] + [(1, u) for u in range(UNITS)]
+            front_a(0, u)
+            gate(0, u)
+        back(0, 0, 0)
+        after_tab = keep.tile([P, 2, PACK, HALF], F32, name="tab_then_wg", align_bytes=64)
+        wg_late = keep.tile([P, PACK, HALF], F32, name="raw_then_wg")
+        wg, raw = [after_tab[:, 0], wg_late[:]], after_tab[:, 1]
+        load_wgs(wg[0][:, :, 0:CHUNK], 0, CHUNK)
+        load_wgs(wg[0][:, :, CHUNK:HALF], CHUNK, HALF)
+        load_raw(raw, w1[:, GROUP : 2 * GROUP])
+        load_wgs(wg[1], HALF, S)
 
-        def advance():
-            g, u = later.pop(0)
-            back(g, u)
-            if len(later) >= 4:
-                front(*later[3])
-
-        for quarter in range(3):
+        rows, pairs = [], []
+        rounds = [(g, quarter) for g in range(GROUPS) for quarter in range(QUARTERS)]
+        for (g, quarter), following in zip(rounds, rounds[1:] + [None]):
+            ahead = [] if following is None else [(following[0], 2 * following[1] + uu) for uu in range(2)]
             for t in range(PACK):
-                scatter(0, t, quarter * CHUNK, (quarter + 1) * CHUNK)
-                if t % 2 == 0:
-                    advance()
-        for t in range(PACK):
-            scatter(0, t, 3 * CHUNK, S)
-            if t > 0:
-                make_z(0, t - 1, 0, M)
-            fetch(0, t, 0, M)
-            while len(later) > 2 * max(2 - t, 0):
-                advance()
-        wo_raw = ring.tile([P, GROUPS, PACK, N], F32, name="wide")
-        for g in range(GROUPS):
-            nc.sync.dma_start(out=wo_raw[:, g], in_=wo[g * GROUP : (g + 1) * GROUP, :].rearrange("(p i) n -> p i n", i=PACK))
-        for t in range(PACK):
-            if t == 0:
-                scatter(1, t, 0, HALF)
-                scatter(1, t, HALF, S)
-            else:
-                scatter(1, t, 0, S)
-            if t == 0:
-                make_z(0, 3, 0, M)
-                for c in range(CHUNKS):
-                    weave_z(nc.scalar.copy, 0, c)
-                wo_staged = [round_wo(wo_raw[:, g]) for g in range(GROUPS)]
-            else:
-                make_z(1, t - 1, 0, M)
-                if t == 1:
-                    for c in range(CHUNKS):
-                        quantize_z(0, c)
                 if t == 2:
-                    for g in range(GROUPS):
-                        quantize(wo_w, wo_s, g, wo_staged[g])
-                    for k in range(M // P):
-                        project(0, k)
-            if t < PACK - 1:
-                fetch(1, t, 0, M)
+                    for unit in ahead:
+                        front_bd(*unit)
+                        gate(*unit)
+                    back(g, quarter, 1)
+                    for unit in ahead:
+                        front_a(*unit)
+                    if following is not None:
+                        back(*following, 0)
+                scatter(g, t, quarter * CHUNK, (quarter + 1) * CHUNK)
+                if (g, quarter) == (0, QUARTERS - 1):
+                    rows.append(fetch_rows(t))
+            if (g, quarter) == (0, 0):
+                quantize(w1_w, w1_s, 1, round_w1(1, raw, 4))
+            elif g == 0 and quarter < 3:
+                gg = quarter - 1
+                load_raw(raw, wo[gg * GROUP : (gg + 1) * GROUP, :])
+                quantize(wo_w, wo_s, gg, round_wo(gg, raw))
+                held_sb[gg] = load_held(gg, f"staged_then_held{gg}")
+            elif (g, quarter) == (1, 0):
+                for t in range(PACK):
+                    nc.scalar.activation(out=rows[t][:], in_=rows[t][:], func=ACT.Copy, scale=gain_sb[:, 0, t : t + 1])
+            elif g == 1 and quarter in (1, 2):
+                pairs.append(add_held_turned(quarter - 1, rows[2 * quarter - 2 : 2 * quarter]))
+            elif g == 1 and quarter == 3:
+                for c in range(CHUNKS):
+                    turn_back(pairs, c)
+                    quantize_z(0, c)
+        for k in range(M // P):
+            project(0, k)
 
         y_sb = ring.tile([P, PACK, M], F32, name="wide")
         y_woven = {}
-        last = PACK - 1
-        x_last = {}
+        x_cols, z_cols = {}, {}
 
         def empty_y(c):
-            y_woven[c] = ring.tile([P, CHUNK * PACK], BF16, name="y_woven", align_bytes=64)
+            y_woven[c] = ring.tile([P, CHUNK * PACK], BF16, name="y_woven", bufs=3, align_bytes=64)
             for e in range(CHUNK // P):
                 k = c * (CHUNK // P) + e
                 project(1, k)
@@ -307,43 +314,53 @@ def tile_list_reshard_resume_features_kernel(
             nc.sync.dma_start(out=out_0.rearrange("(p t) m -> p t m", t=PACK)[:, :, cols], in_=y_sb[:, :, cols])
 
         def weave_y(c):
-            nc.vector.tensor_copy(
-                out=y_woven[c][:].rearrange("p (m e t) -> p m t e", e=4, t=PACK),
-                in_=y_sb[:, :, c * CHUNK : (c + 1) * CHUNK].rearrange("p t (m e) -> p m t e", e=4),
-            )
+            if c in YS:
+                for e in range(CHUNK // P):
+                    nc.scalar.copy(
+                        out=y_woven[c][:, e * GROUP : (e + 1) * GROUP].rearrange("p (m t) -> p m t", t=PACK),
+                        in_=y_bank[c * (CHUNK // P) + e][:].rearrange("p t m -> p m t"),
+                    )
+            else:
+                nc.vector.tensor_copy(
+                    out=y_woven[c][:].rearrange("p (m e t) -> p m t e", e=4, t=PACK),
+                    in_=y_sb[:, :, c * CHUNK : (c + 1) * CHUNK].rearrange("p t (m e) -> p m t e", e=4),
+                )
 
         def quantize_y(c):
             cols = slice(c * CHUNK, (c + 1) * CHUNK)
             nc.vector.quantize_mx(out=y_w[:, cols].bitcast(FP8X4), scales=y_s[:, cols], in_=y_woven[c][:])
             nc.sync.dma_start(out=out_1[0].rearrange("p m t -> p (m t)").bitcast(I32)[:, cols], in_=y_w[:, cols].bitcast(I32))
 
-        def fetch_last(c):
-            if c < 2:
-                x = xs[last % 2][:, c * CHUNK : (c + 1) * CHUNK]
-            else:
-                x = keep.tile([P, CHUNK], F32, name=f"z_woven{c - 2}", align_bytes=64)[:]
-            x_last[c] = x
-            nc.vector.tensor_copy(x, page_of(1, last)[:].indirect(list3[:, c * CHUNK // PER_COL : (c + 1) * CHUNK // PER_COL]))
-            nc.scalar.activation(out=x, in_=x, func=ACT.Silu)
+        def fetch_cols(c):
+            x_cols[c] = keep.tile([P, PACK, CHUNK], F32, name=f"x{2 + c % 2}")
+            for t in range(PACK):
+                nc.vector.tensor_copy(x_cols[c][:, t, :], pages[t][:].indirect(list3[:, c * CHUNK // PER_COL : (c + 1) * CHUNK // PER_COL]))
+            nc.scalar.activation(out=x_cols[c][:], in_=x_cols[c][:], func=ACT.Silu)
 
-        def make_last(c):
-            cols = slice(c * CHUNK, (c + 1) * CHUNK)
-            nc.vector.scalar_tensor_tensor(
-                out=z_rows[1][:, last, cols], in0=x_last[c],
-                scalar=gain_sb[:, 1, last : last + 1], in1=held_sb[1][:, last, cols], op0=MULT, op1=ADD,
+        def make_z(c):
+            z_cols[c] = ring.tile([P, PACK, CHUNK], BF16, name="z_cols")
+            for t in range(PACK):
+                nc.vector.scalar_tensor_tensor(
+                    out=z_cols[c][:, t, :], in0=x_cols[c][:, t, :], scalar=gain_sb[:, 1, t : t + 1],
+                    in1=held_sb[1][:, t, c * CHUNK : (c + 1) * CHUNK], op0=MULT, op1=ADD,
+                )
+            (nc.scalar.copy if c in ZS else nc.vector.tensor_copy)(
+                out=new_woven(1, c)[:].rearrange("p (m e t) -> p m t e", e=4, t=PACK),
+                in_=z_cols[c][:].rearrange("p t (m e) -> p m t e", e=4),
             )
 
-        fetch_last(0)
-        fetch_last(1)
+        fetch_cols(0)
+        fetch_cols(1)
         for c in range(CHUNKS):
-            make_last(c)
-            weave_z(nc.scalar.copy if c == 1 else nc.vector.tensor_copy, 1, c)
-            quantize_z(1, c)
+            make_z(c)
             if c + 2 < CHUNKS:
-                fetch_last(c + 2)
-        for c in range(CHUNKS):
+                fetch_cols(c + 2)
+            quantize_z(1, c)
+            if c >= LAG:
+                quantize_y(c - LAG)
             empty_y(c)
             weave_y(c)
+        for c in range(CHUNKS - LAG, CHUNKS):
             quantize_y(c)
         for q in range(4):
             nc.sync.dma_start(out=out_2[0, 4 * q : 4 * q + 4, :].bitcast(I32), in_=y_s[32 * q : 32 * q + 4, :].bitcast(I32))

@@ -55,15 +55,12 @@ def tile_list_reshard_resume_features_kernel(
         w2_s = keep.tile([P, H], U8, name="w2_s", align_bytes=64)
         w3_w = keep.tile([P, H], U32, name="w3_w", align_bytes=64)
         w3_s = keep.tile([P, H], U8, name="w3_s", align_bytes=64)
-        wo_w = keep.tile([P, GROUPS * N], U32, name="wo_w", align_bytes=64)
         wo_s = keep.tile([P, GROUPS * N], U8, name="wo_s", align_bytes=64)
-        z_w = keep.tile([P, GROUPS * M], U32, name="z_w", align_bytes=64)
         z_s = keep.tile([P, GROUPS * M], U8, name="z_s", align_bytes=64)
         y_w = keep.tile([P, M], U32, name="y_w", align_bytes=64)
         y_s = keep.tile([P, M], U8, name="y_s", align_bytes=64)
-        gain_sb = keep.tile([P, GROUPS, PACK], F32, name="gain_sb")
         ident = keep.tile([P, P], F32, name="ident")
-        pages = [keep.tile([P, T2], F32, name=f"page{t}") for t in range(PACK)]
+        pages = [keep.tile([P, T2], F32, name=f"page{t}") for t in range(2)]
 
         def load_scales(queue, plane, rows, quadrants):
             for q in quadrants:
@@ -98,12 +95,9 @@ def tile_list_reshard_resume_features_kernel(
         load_scales(nc.gpsimd, w2_s, w2_scales, range(3))
         load_scales(nc.scalar, w2_s, w2_scales, range(3, 4))
         make_identity(nc, ident[:])
-        for page in pages[:2]:
+        for page in pages:
             nc.vector.memset(page[:, : T2 // 2 - 1], 0.0)
             nc.vector.memset(page[:, T2 // 2 - 1 :], 0.0)
-        for page in pages[2:]:
-            nc.gpsimd.memset(page[:], 0.0)
-        nc.gpsimd.dma_start(out=gain_sb[:], in_=gain.rearrange("(g p t) -> p g t", p=P, t=PACK))
 
         def gather_table(half):
             cols = slice(half * HALF, (half + 1) * HALF)
@@ -111,18 +105,13 @@ def tile_list_reshard_resume_features_kernel(
             nc.vector.tensor_copy(v_w[:, cols], tab_w[:].indirect(entries))
             nc.vector.tensor_copy(v_s[:, cols], tab_s[:].indirect(entries))
 
-        def round_w1(g, raw, pieces):
-            staged = keep.tile([P, GROUP * PACK], BF16, name=f"staged_then_held{g}", align_bytes=64)
-            width = GROUP // pieces
-            for c in range(pieces):
-                nc.scalar.copy(
-                    out=staged[:, c * width * PACK : (c + 1) * width * PACK].rearrange("p (c e i) -> p c i e", e=4, i=PACK),
-                    in_=raw[:, :, c * width : (c + 1) * width].rearrange("p i (c e) -> p c i e", e=4),
-                )
-            return staged
+        def round_w1(staged, raw):
+            nc.scalar.copy(
+                out=staged.rearrange("p (c e i) -> p c i e", e=4, i=PACK), in_=raw.rearrange("p i (c e) -> p c i e", e=4)
+            )
 
         def round_wo(g, raw):
-            staged = keep.tile([P, GROUP * PACK], BF16, name=f"staged_then_held{g}", align_bytes=64)
+            staged = keep.tile([P, GROUP * PACK], BF16, name=("w3_s", "w1_s")[g], align_bytes=64)
             width = P // 4
             for c in range(4):
                 nc.scalar.copy(
@@ -147,21 +136,26 @@ def tile_list_reshard_resume_features_kernel(
 
         b_bank, tanh_d, a_sb, h_sb = {}, {}, {}, {}
 
+        b_sb = {}
+
+        def on_gpsimd(g, u):
+            return (g, u) > (0, 1)
+
         def front_bd(g, u):
             cols = slice(g * GROUP, (g + 1) * GROUP)
-            if u % 2 == 1:
-                d_bank = psum.tile([P, GROUP], F32, name="chain_bank")
-            else:
-                d_bank = psum.tile([P, GROUP], F32, name="ad_bank", bufs=2)
+            d_bank = psum.tile([P, GROUP], F32, name="ad_bank", bufs=3)
             product(d_bank, u, w3_w[:, cols].bitcast(FP8X4), w3_s[:, cols])
             b_bank[g, u] = psum.tile([P, GROUP], F32, name="b_bank", bufs=2)
             product(b_bank[g, u], u, w2_w[:, 2 * g * GROUP : 2 * (g + 1) * GROUP].bitcast(FP4X4), w2_s[:, cols])
             tanh_d[g, u] = ring.tile([P, PACK, P], F32, name="tanh_d", bufs=2)
             nc.scalar.activation(out=tanh_d[g, u][:], in_=dealt(d_bank), func=ACT.Tanh)
+            if on_gpsimd(g, u):
+                b_sb[g, u] = ring.tile([P, PACK, P], F32, name="b_sb", bufs=2)
+                nc.scalar.copy(out=b_sb[g, u][:], in_=dealt(b_bank[g, u]))
 
         def front_a(g, u):
             cols = slice(g * GROUP, (g + 1) * GROUP)
-            a_bank = psum.tile([P, GROUP], F32, name="ad_bank", bufs=2)
+            a_bank = psum.tile([P, GROUP], F32, name="ad_bank", bufs=3)
             product(a_bank, u, w1_w[:, cols].bitcast(FP8X4), w1_s[:, cols])
             a_sb[g, u] = ring.tile([P, PACK, P], F32, name="a_sb", bufs=4)
             nc.scalar.copy(out=a_sb[g, u][:], in_=dealt(a_bank))
@@ -169,16 +163,21 @@ def tile_list_reshard_resume_features_kernel(
         gated = {}
 
         def gate(g, u):
-            gated[g, u] = ring.tile([P, PACK, P], F32, name="gated", bufs=4)
-            nc.vector.tensor_tensor(gated[g, u][:], dealt(b_bank[g, u]), tanh_d[g, u][:], MULT)
+            if (g, u) == (0, 1):
+                gated[g, u] = keep.tile([P, PACK, P], F32, name="then_held0", align_bytes=64)
+            else:
+                gated[g, u] = ring.tile([P, PACK, P], F32, name="gated", bufs=4)
+            if on_gpsimd(g, u):
+                for e in range(1):
+                    part = slice(e * PACK // 1, (e + 1) * PACK // 1)
+                    nc.gpsimd.tensor_tensor(gated[g, u][:, part], b_sb[g, u][:, part], tanh_d[g, u][:, part], MULT)
+            else:
+                nc.vector.tensor_tensor(gated[g, u][:], dealt(b_bank[g, u]), tanh_d[g, u][:], MULT)
 
         def back(g, quarter, pair):
             if (quarter, pair) == (0, 0):
-                h_sb[g] = ring.tile([P, PACK, S], F32, name="wide")
-            if pair == 0:
-                h_bank = psum.tile([P, 2, CHUNK], F32, name="turn_bank", bufs=3)
-            else:
-                h_bank = psum.tile([P, 2, CHUNK], F32, name="chain_bank")
+                h_sb[g] = keep.tile([P, PACK, S], F32, name=f"wide{g}", align_bytes=64)
+            h_bank = psum.tile([P, 2, CHUNK], F32, name="turn_bank", bufs=3)
             if True:
                 for e in range(2):
                     for uu in range(2):
@@ -187,10 +186,15 @@ def tile_list_reshard_resume_features_kernel(
                         nc.tensor.matmul(out, a_sb[g, u][:, t, :], ident[:], start=True, stop=False, is_transpose=True)
                         nc.tensor.matmul(out, gated[g, u][:, t, :], ident[:], start=False, stop=True, is_transpose=True)
                 nc.scalar.copy(out=h_sb[g][:, 2 * pair : 2 * pair + 2, quarter * CHUNK : (quarter + 1) * CHUNK], in_=h_bank[:])
+                lo = quarter * CHUNK
+                for e in range(1):
+                    part = slice(2 * pair + e * 2 // 1, 2 * pair + (e + 1) * 2 // 1)
+                    both = h_sb[g][:, part, lo : lo + CHUNK]
+                    nc.gpsimd.tensor_tensor(both, both, wg[lo // HALF][:, part, lo % HALF : lo % HALF + CHUNK], MULT)
 
         def scatter(g, t, lo, hi):
             entries = list2[:, lo // PER_COL : hi // PER_COL]
-            nc.vector.tensor_tensor(pages[t][:].indirect(entries), h_sb[g][:, t, lo:hi], wg[lo // HALF][:, t, lo % HALF : lo % HALF + hi - lo], MULT)
+            nc.vector.tensor_copy(pages[t][:].indirect(entries), h_sb[g][:, t, lo:hi])
 
         held_sb, z_woven = {}, {}
 
@@ -201,7 +205,6 @@ def tile_list_reshard_resume_features_kernel(
         def fetch_rows(t):
             x = keep.tile([P, M], F32, name=f"x{t}")
             nc.vector.tensor_copy(x[:], pages[t][:].indirect(list3[:]))
-            nc.scalar.activation(out=x[:], in_=x[:], func=ACT.Silu)
             return x
 
         def add_held_turned(pair, rows):
@@ -234,7 +237,7 @@ def tile_list_reshard_resume_features_kernel(
 
         def project(g, k):
             if g == 0:
-                tag, bufs = ([("b_bank", 2)] * 2 + [("ad_bank", 2)] * 2 + [("chain_bank", 1)] + [("turn_bank", 3)] * 3)[k]
+                tag, bufs = ([("b_bank", 2)] * 2 + [("ad_bank", 3)] * 3 + [("turn_bank", 3)] * 3)[k]
                 y_bank[k] = psum.tile([P, PACK, P], F32, name=tag, bufs=bufs)
             cols = slice(g * M + k * P, g * M + (k + 1) * P)
             for t in range(PACK):
@@ -247,60 +250,87 @@ def tile_list_reshard_resume_features_kernel(
 
         gather_table(0)
         gather_table(1)
-        staged = round_w1(0, raw_first[:], 1)
+        halves = []
+        for e in range(2):
+            halves.append(keep.tile([P, CHUNK * PACK], BF16, name=f"staged_then_page{e}", align_bytes=64))
+            round_w1(halves[e][:], raw_first[:, :, e * CHUNK : (e + 1) * CHUNK])
         for u in range(2):
             front_bd(0, u)
         w1_w = keep.tile([P, H], U32, name="tab_s_then_w1", align_bytes=64)
-        quantize(w1_w, w1_s, 0, staged)
+        for e in range(2):
+            cols = slice(e * CHUNK, (e + 1) * CHUNK)
+            nc.vector.quantize_mx(out=w1_w[:, cols].bitcast(FP8X4), scales=w1_s[:, cols], in_=halves[e][:])
         for u in range(2):
             front_a(0, u)
             gate(0, u)
-        back(0, 0, 0)
-        after_tab = keep.tile([P, 2, PACK, HALF], F32, name="tab_then_wg", align_bytes=64)
+        for e in range(2):
+            pages.append(keep.tile([P, T2], F32, name=f"staged_then_page{e}", align_bytes=64))
+            nc.vector.memset(pages[2 + e][:], 0.0)
+        after_tab = keep.tile([P, 2 * PACK * HALF + GROUPS * PACK], F32, name="tab_then_wg", align_bytes=64)
         wg_late = keep.tile([P, PACK, HALF], F32, name="raw_then_wg")
-        wg, raw = [after_tab[:, 0], wg_late[:]], after_tab[:, 1]
+        wg = [after_tab[:, : PACK * HALF].rearrange("p (t j) -> p t j", t=PACK), wg_late[:]]
+        raw = after_tab[:, PACK * HALF : 2 * PACK * HALF].rearrange("p (i c) -> p i c", i=PACK)
+        gain_sb = after_tab[:, 2 * PACK * HALF :].rearrange("p (g t) -> p g t", t=PACK)
         load_wgs(wg[0][:, :, 0:CHUNK], 0, CHUNK)
         load_wgs(wg[0][:, :, CHUNK:HALF], CHUNK, HALF)
         load_raw(raw, w1[:, GROUP : 2 * GROUP])
+        nc.sync.dma_start(out=gain_sb, in_=gain.rearrange("(g p t) -> p g t", p=P, t=PACK))
         load_wgs(wg[1], HALF, S)
 
-        rows, pairs = [], []
+        back(0, 0, 0)
+        rows = []
         rounds = [(g, quarter) for g in range(GROUPS) for quarter in range(QUARTERS)]
-        for (g, quarter), following in zip(rounds, rounds[1:] + [None]):
-            ahead = [] if following is None else [(following[0], 2 * following[1] + uu) for uu in range(2)]
+
+        def fronts(r):
+            g, quarter = rounds[r]
+            for u in (2 * quarter, 2 * quarter + 1):
+                front_bd(g, u)
+                gate(g, u)
+                front_a(g, u)
+
+        for r, (g, quarter) in enumerate(rounds):
+            if r == 0:
+                back(g, quarter, 1)
+                fronts(1)
+            if 0 == 0 and r + 2 < len(rounds):
+                fronts(r + 2)
+            if r + 1 < len(rounds):
+                back(*rounds[r + 1], 0)
+                back(*rounds[r + 1], 1)
+            if 0 == 1 and r + 2 < len(rounds):
+                fronts(r + 2)
             for t in range(PACK):
-                if t == 2:
-                    for unit in ahead:
-                        front_bd(*unit)
-                        gate(*unit)
-                    back(g, quarter, 1)
-                    for unit in ahead:
-                        front_a(*unit)
-                    if following is not None:
-                        back(*following, 0)
                 scatter(g, t, quarter * CHUNK, (quarter + 1) * CHUNK)
                 if (g, quarter) == (0, QUARTERS - 1):
                     rows.append(fetch_rows(t))
-            if (g, quarter) == (0, 0):
-                quantize(w1_w, w1_s, 1, round_w1(1, raw, 4))
-            elif g == 0 and quarter < 3:
-                gg = quarter - 1
-                load_raw(raw, wo[gg * GROUP : (gg + 1) * GROUP, :])
-                quantize(wo_w, wo_s, gg, round_wo(gg, raw))
-                held_sb[gg] = load_held(gg, f"staged_then_held{gg}")
-            elif (g, quarter) == (1, 0):
-                for t in range(PACK):
-                    nc.scalar.activation(out=rows[t][:], in_=rows[t][:], func=ACT.Copy, scale=gain_sb[:, 0, t : t + 1])
-            elif g == 1 and quarter in (1, 2):
-                pairs.append(add_held_turned(quarter - 1, rows[2 * quarter - 2 : 2 * quarter]))
-            elif g == 1 and quarter == 3:
-                for c in range(CHUNKS):
-                    turn_back(pairs, c)
-                    quantize_z(0, c)
+            if r == 0:
+                staged = keep.tile([P, GROUP * PACK], BF16, name="then_held0", align_bytes=64)
+                for c in range(4):
+                    round_w1(staged[:, c * GROUP : (c + 1) * GROUP], raw[:, :, c * P : (c + 1) * P])
+                quantize(w1_w, w1_s, 1, staged)
+                held_sb[0] = load_held(0, "then_held0")
+                load_raw(raw, wo[0:GROUP, :])
+        held_sb[1] = load_held(1, "w2_s")
+        codes = keep.tile([P, GROUPS * (N + M)], U32, name="wide1", align_bytes=64)
+        wo_w, z_w = codes[:, : GROUPS * N], codes[:, GROUPS * N :]
+        pairs = []
+        for pair in range(2):
+            active = []
+            for t in (2 * pair, 2 * pair + 1):
+                active.append(keep.tile([P, M], F32, name=("v_w", "w3_w", "tab_s_then_w1", "w2_w")[t], align_bytes=64))
+                nc.scalar.activation(out=active[-1][:], in_=rows[t][:], func=ACT.Silu)
+                nc.scalar.activation(out=active[-1][:], in_=active[-1][:], func=ACT.Copy, scale=gain_sb[:, 0, t : t + 1])
+            pairs.append(add_held_turned(pair, active))
+            quantize(wo_w, wo_s, pair, round_wo(pair, raw))
+            if pair == 0:
+                load_raw(raw, wo[GROUP : 2 * GROUP, :])
+        for c in range(CHUNKS):
+            turn_back(pairs, c)
+            quantize_z(0, c)
         for k in range(M // P):
             project(0, k)
 
-        y_sb = ring.tile([P, PACK, M], F32, name="wide")
+        y_sb = keep.tile([P, PACK, M], F32, name="wide0", align_bytes=64)
         y_woven = {}
         x_cols, z_cols = {}, {}
 
@@ -332,7 +362,7 @@ def tile_list_reshard_resume_features_kernel(
             nc.sync.dma_start(out=out_1[0].rearrange("p m t -> p (m t)").bitcast(I32)[:, cols], in_=y_w[:, cols].bitcast(I32))
 
         def fetch_cols(c):
-            x_cols[c] = keep.tile([P, PACK, CHUNK], F32, name=f"x{2 + c % 2}")
+            x_cols[c] = keep.tile([P, PACK, CHUNK], F32, name=f"turned{c % 2}")
             for t in range(PACK):
                 nc.vector.tensor_copy(x_cols[c][:, t, :], pages[t][:].indirect(list3[:, c * CHUNK // PER_COL : (c + 1) * CHUNK // PER_COL]))
             nc.scalar.activation(out=x_cols[c][:], in_=x_cols[c][:], func=ACT.Silu)

@@ -22,15 +22,16 @@ P = 128
 PACK = 4
 GROUP = P * PACK
 GROUPS = H // GROUP
-UNITS = S // P
+QUADRANTS = 4
+PER_COL = 16
 HALF = S // 2
+QUARTER = S // 4
+QUARTERS = S // QUARTER
 CHUNK = 256
 CHUNKS = M // CHUNK
-QUARTERS = S // CHUNK
-PER_COL = 16
-ZS = (0, 1)
-YS = (0, 1)
-LAG = 1
+NEIGHBOURS = 4
+VECTOR_UNITS = 2
+SCALAR_WEAVES = 2
 
 
 def tile_list_reshard_resume_features_kernel(
@@ -46,83 +47,78 @@ def tile_list_reshard_resume_features_kernel(
         list1 = keep.tile([P, S // PER_COL], U16, name="list1")
         list2 = keep.tile([P, S // PER_COL], U16, name="list2")
         list3 = keep.tile([P, M // PER_COL], U16, name="list3")
-        tab_w = keep.tile([P, T], U32, name="tab_then_wg", align_bytes=64)
-        tab_s = keep.tile([P, T], U8, name="tab_s_then_w1", align_bytes=64)
-        v_w = keep.tile([P, S], U32, name="v_w", align_bytes=64)
+        tab_w = keep.tile([P, T], U32, name="tab_w_then_factors", align_bytes=64)
+        tab_s = keep.tile([P, T], U8, name="tab_s_then_w1_then_active", align_bytes=64)
+        v_w = keep.tile([P, S], U32, name="v_w_then_active", align_bytes=64)
         v_s = keep.tile([P, S], U8, name="v_s", align_bytes=64)
-        w1_s = keep.tile([P, H], U8, name="w1_s", align_bytes=64)
-        w2_w = keep.tile([P, 2 * H], U8, name="w2_w", align_bytes=64)
-        w2_s = keep.tile([P, H], U8, name="w2_s", align_bytes=64)
-        w3_w = keep.tile([P, H], U32, name="w3_w", align_bytes=64)
-        w3_s = keep.tile([P, H], U8, name="w3_s", align_bytes=64)
-        wo_s = keep.tile([P, GROUPS * N], U8, name="wo_s", align_bytes=64)
+        w1_s = keep.tile([P, H], U8, name="w1_s_then_wo1", align_bytes=64)
+        w2_w = keep.tile([P, 2 * H], U8, name="w2_w_then_active", align_bytes=64)
+        w2_s = keep.tile([P, H], U8, name="w2_s_then_held1", align_bytes=64)
+        w3_w = keep.tile([P, H], U32, name="w3_w_then_active", align_bytes=64)
+        w3_s = keep.tile([P, H], U8, name="w3_s_then_wo0", align_bytes=64)
         z_s = keep.tile([P, GROUPS * M], U8, name="z_s", align_bytes=64)
         y_w = keep.tile([P, M], U32, name="y_w", align_bytes=64)
         y_s = keep.tile([P, M], U8, name="y_s", align_bytes=64)
         ident = keep.tile([P, P], F32, name="ident")
         pages = [keep.tile([P, T2], F32, name=f"page{t}") for t in range(2)]
 
-        def load_scales(queue, plane, rows, quadrants):
+        def load_scales(queue, plane, scales, quadrants):
             for q in quadrants:
-                queue.dma_start(out=plane[32 * q : 32 * q + 4, :].bitcast(I32), in_=rows[0, 4 * q : 4 * q + 4, :].bitcast(I32))
+                queue.dma_start(out=plane[32 * q : 32 * q + 4, :].bitcast(I32), in_=scales[0, 4 * q : 4 * q + 4, :].bitcast(I32))
 
-        def load_raw(raw, rows):
-            nc.sync.dma_start(out=raw, in_=rows.rearrange("(p i) c -> p i c", i=PACK))
-            return raw
+        def load_weight(raw, weight):
+            nc.sync.dma_start(out=raw, in_=weight.rearrange("(p i) c -> p i c", i=PACK))
 
         def load_wgs(part, lo, hi):
             for q in (0, 2, 1, 3):
                 nc.sync.dma_start(out=part[32 * q : 32 * q + 32], in_=wgs.rearrange("(p t) j -> p t j", t=PACK)[:, :, lo:hi])
 
-        def load_held(g, tag):
-            rows = keep.tile([P, PACK, M], F32, name=tag, align_bytes=64)
-            nc.sync.dma_start(out=rows[:], in_=held[g * GROUP : (g + 1) * GROUP, :].rearrange("(p t) m -> p t m", t=PACK))
-            return rows
+        def load_held(g, name):
+            dealt_held = keep.tile([P, PACK, M], F32, name=name, align_bytes=64)
+            nc.sync.dma_start(out=dealt_held[:], in_=held[g * GROUP : (g + 1) * GROUP, :].rearrange("(p t) m -> p t m", t=PACK))
+            return dealt_held
 
         nc.sync.dma_start(list1[:], offs)
         nc.sync.dma_start(list2[:], offs2)
         nc.sync.dma_start(list3[:], offs3)
         nc.sync.dma_start(out=tab_w[:].bitcast(I32), in_=tab_words[0].rearrange("p t i -> p (t i)").bitcast(I32))
-        raw_first = keep.tile([P, PACK, GROUP], F32, name="raw_then_wg")
-        load_raw(raw_first[:], w1[:, 0:GROUP])
+        w1_raw0 = keep.tile([P, PACK, GROUP], F32, name="w1_raw0_then_wgs")
+        load_weight(w1_raw0[:], w1[:, 0:GROUP])
         nc.sync.dma_start(out=w3_w[:].bitcast(I32), in_=w3_words[0].rearrange("p c i -> p (c i)").bitcast(I32))
         nc.sync.dma_start(out=w2_w[:].bitcast(I32), in_=w2_words[0].bitcast(I32))
         nc.vector.memset(tab_s[:].bitcast(I32), 0)
-        load_scales(nc.scalar, tab_s, tab_scales, range(4))
+        load_scales(nc.scalar, tab_s, tab_scales, range(QUADRANTS))
         nc.gpsimd.memset(w3_s[:].bitcast(I32), 0)
-        load_scales(nc.gpsimd, w3_s, w3_scales, range(4))
+        load_scales(nc.gpsimd, w3_s, w3_scales, range(QUADRANTS))
         nc.vector.memset(w2_s[:].bitcast(I32), 0)
-        load_scales(nc.gpsimd, w2_s, w2_scales, range(3))
-        load_scales(nc.scalar, w2_s, w2_scales, range(3, 4))
+        load_scales(nc.gpsimd, w2_s, w2_scales, range(QUADRANTS - 1))
+        load_scales(nc.scalar, w2_s, w2_scales, [QUADRANTS - 1])
         make_identity(nc, ident[:])
         for page in pages:
             nc.vector.memset(page[:, : T2 // 2 - 1], 0.0)
             nc.vector.memset(page[:, T2 // 2 - 1 :], 0.0)
 
-        def gather_table(half):
-            cols = slice(half * HALF, (half + 1) * HALF)
-            entries = list1[:, half * HALF // PER_COL : (half + 1) * HALF // PER_COL]
-            nc.vector.tensor_copy(v_w[:, cols], tab_w[:].indirect(entries))
-            nc.vector.tensor_copy(v_s[:, cols], tab_s[:].indirect(entries))
-
-        def round_w1(staged, raw):
+        def round_w1(woven, raw):
             nc.scalar.copy(
-                out=staged.rearrange("p (c e i) -> p c i e", e=4, i=PACK), in_=raw.rearrange("p i (c e) -> p c i e", e=4)
+                out=woven.rearrange("p (c e i) -> p c i e", e=NEIGHBOURS, i=PACK),
+                in_=raw.rearrange("p i (c e) -> p c i e", e=NEIGHBOURS),
             )
 
-        def round_wo(g, raw):
-            staged = keep.tile([P, GROUP * PACK], BF16, name=("w3_s", "w1_s")[g], align_bytes=64)
-            width = P // 4
-            for c in range(4):
+        def round_wo(raw, name):
+            woven = keep.tile([P, GROUP * PACK], BF16, name=name, align_bytes=64)
+            width = P // PACK
+            for piece in range(PACK):
+                cols = slice(piece * width, (piece + 1) * width)
                 nc.scalar.copy(
-                    out=staged[:].rearrange("p (t c i) -> p c t i", t=PACK, i=PACK)[:, c * width : (c + 1) * width],
-                    in_=raw.rearrange("p i (c t) -> p c t i", t=PACK)[:, c * width : (c + 1) * width],
+                    out=woven[:].rearrange("p (t c i) -> p c t i", t=PACK, i=PACK)[:, cols],
+                    in_=raw.rearrange("p i (c t) -> p c t i", t=PACK)[:, cols],
                 )
-            return staged
+            return woven
 
-        def quantize(words, scales, g, staged):
-            cols = slice(g * GROUP, (g + 1) * GROUP)
-            nc.vector.quantize_mx(out=words[:, cols].bitcast(FP8X4), scales=scales[:, cols], in_=staged[:])
+        def quantize(words, scales, cols, woven):
+            nc.vector.quantize_mx(out=words[:, cols].bitcast(FP8X4), scales=scales[:, cols], in_=woven[:])
+
+        b_bank, b_sb, tanh_d, a_sb, gated, h_sb = {}, {}, {}, {}, {}, {}
 
         def dealt(bank):
             return bank[:].rearrange("j (p t) -> j t p", t=PACK)
@@ -134,263 +130,272 @@ def tile_list_reshard_resume_features_kernel(
                 rhs=moving, rhs_scale=moving_scales, start=True, stop=True,
             )
 
-        b_bank, tanh_d, a_sb, h_sb = {}, {}, {}, {}
+        def on_vector(g, u):
+            return g == 0 and u < VECTOR_UNITS
 
-        b_sb = {}
-
-        def on_gpsimd(g, u):
-            return (g, u) > (0, 1)
-
-        def front_bd(g, u):
+        def products_d_b(g, u):
             cols = slice(g * GROUP, (g + 1) * GROUP)
             d_bank = psum.tile([P, GROUP], F32, name="ad_bank", bufs=3)
             product(d_bank, u, w3_w[:, cols].bitcast(FP8X4), w3_s[:, cols])
             b_bank[g, u] = psum.tile([P, GROUP], F32, name="b_bank", bufs=2)
             product(b_bank[g, u], u, w2_w[:, 2 * g * GROUP : 2 * (g + 1) * GROUP].bitcast(FP4X4), w2_s[:, cols])
-            tanh_d[g, u] = ring.tile([P, PACK, P], F32, name="tanh_d", bufs=2)
+            tanh_d[g, u] = ring.tile([P, PACK, P], F32, name="tanh_d")
             nc.scalar.activation(out=tanh_d[g, u][:], in_=dealt(d_bank), func=ACT.Tanh)
-            if on_gpsimd(g, u):
-                b_sb[g, u] = ring.tile([P, PACK, P], F32, name="b_sb", bufs=2)
+            if not on_vector(g, u):
+                b_sb[g, u] = ring.tile([P, PACK, P], F32, name="b_sb")
                 nc.scalar.copy(out=b_sb[g, u][:], in_=dealt(b_bank[g, u]))
 
-        def front_a(g, u):
+        def product_a(g, u):
             cols = slice(g * GROUP, (g + 1) * GROUP)
             a_bank = psum.tile([P, GROUP], F32, name="ad_bank", bufs=3)
             product(a_bank, u, w1_w[:, cols].bitcast(FP8X4), w1_s[:, cols])
             a_sb[g, u] = ring.tile([P, PACK, P], F32, name="a_sb", bufs=4)
             nc.scalar.copy(out=a_sb[g, u][:], in_=dealt(a_bank))
 
-        gated = {}
-
         def gate(g, u):
             if (g, u) == (0, 1):
-                gated[g, u] = keep.tile([P, PACK, P], F32, name="then_held0", align_bytes=64)
+                gated[g, u] = keep.tile([P, PACK, P], F32, name="gated_then_w1_then_held0", align_bytes=64)
             else:
                 gated[g, u] = ring.tile([P, PACK, P], F32, name="gated", bufs=4)
-            if on_gpsimd(g, u):
-                for e in range(1):
-                    part = slice(e * PACK // 1, (e + 1) * PACK // 1)
-                    nc.gpsimd.tensor_tensor(gated[g, u][:, part], b_sb[g, u][:, part], tanh_d[g, u][:, part], MULT)
-            else:
+            if on_vector(g, u):
                 nc.vector.tensor_tensor(gated[g, u][:], dealt(b_bank[g, u]), tanh_d[g, u][:], MULT)
+            else:
+                nc.gpsimd.tensor_tensor(gated[g, u][:], b_sb[g, u][:], tanh_d[g, u][:], MULT)
 
-        def back(g, quarter, pair):
+        def add_turned(out, first, second):
+            nc.tensor.matmul(out, first, ident[:], start=True, stop=False, is_transpose=True)
+            nc.tensor.matmul(out, second, ident[:], start=False, stop=True, is_transpose=True)
+
+        def factors(slots, lo, hi):
+            return wg[lo // HALF][:, slots, lo % HALF : lo % HALF + hi - lo]
+
+        def make_h(g, quarter, pair):
             if (quarter, pair) == (0, 0):
-                h_sb[g] = keep.tile([P, PACK, S], F32, name=f"wide{g}", align_bytes=64)
-            h_bank = psum.tile([P, 2, CHUNK], F32, name="turn_bank", bufs=3)
-            if True:
-                for e in range(2):
-                    for uu in range(2):
-                        u, t = 2 * quarter + uu, 2 * pair + e
-                        out = h_bank[:, e, uu * P : (uu + 1) * P]
-                        nc.tensor.matmul(out, a_sb[g, u][:, t, :], ident[:], start=True, stop=False, is_transpose=True)
-                        nc.tensor.matmul(out, gated[g, u][:, t, :], ident[:], start=False, stop=True, is_transpose=True)
-                nc.scalar.copy(out=h_sb[g][:, 2 * pair : 2 * pair + 2, quarter * CHUNK : (quarter + 1) * CHUNK], in_=h_bank[:])
-                lo = quarter * CHUNK
-                for e in range(1):
-                    part = slice(2 * pair + e * 2 // 1, 2 * pair + (e + 1) * 2 // 1)
-                    both = h_sb[g][:, part, lo : lo + CHUNK]
-                    nc.gpsimd.tensor_tensor(both, both, wg[lo // HALF][:, part, lo % HALF : lo % HALF + CHUNK], MULT)
+                h_sb[g] = keep.tile([P, PACK, S], F32, name=("h0_then_y", "h1_then_codes")[g], align_bytes=64)
+            h_bank = psum.tile([P, 2, QUARTER], F32, name="turn_bank", bufs=3)
+            for e in range(2):
+                for side in range(2):
+                    u, t = 2 * quarter + side, 2 * pair + e
+                    add_turned(h_bank[:, e, side * P : (side + 1) * P], a_sb[g, u][:, t, :], gated[g, u][:, t, :])
+            slots, lo, hi = slice(2 * pair, 2 * pair + 2), quarter * QUARTER, (quarter + 1) * QUARTER
+            nc.scalar.copy(out=h_sb[g][:, slots, lo:hi], in_=h_bank[:])
+            if g == 0:
+                nc.gpsimd.tensor_tensor(h_sb[g][:, slots, lo:hi], h_sb[g][:, slots, lo:hi], factors(slots, lo, hi), MULT)
 
-        def scatter(g, t, lo, hi):
-            entries = list2[:, lo // PER_COL : hi // PER_COL]
-            nc.vector.tensor_copy(pages[t][:].indirect(entries), h_sb[g][:, t, lo:hi])
+        def scatter(page, g, t, lo, hi):
+            window = page[:].indirect(list2[:, lo // PER_COL : hi // PER_COL])
+            if g == 0:
+                nc.vector.tensor_copy(window, h_sb[g][:, t, lo:hi])
+            else:
+                nc.vector.tensor_tensor(window, h_sb[g][:, t, lo:hi], factors(t, lo, hi), MULT)
 
-        held_sb, z_woven = {}, {}
-
-        def new_woven(g, c):
-            z_woven[g, c] = ring.tile([P, CHUNK * PACK], BF16, name="z_woven", bufs=CHUNKS, align_bytes=64)
-            return z_woven[g, c]
-
-        def fetch_rows(t):
-            x = keep.tile([P, M], F32, name=f"x{t}")
+        def fetch_slot(t):
+            x = keep.tile([P, M], F32, name=("x0", "x1", "x2_then_turned_then_wo_s", "x3")[t], align_bytes=64)
             nc.vector.tensor_copy(x[:], pages[t][:].indirect(list3[:]))
             return x
 
-        def add_held_turned(pair, rows):
-            turned = keep.tile([P, M // P, P, 2], BF16, name=f"turned{pair}")
+        held_sb, z_woven = {}, {}
+
+        def activate(x, g, t, name):
+            active = keep.tile([P, M], F32, name=name, align_bytes=64)
+            nc.scalar.activation(out=active[:], in_=x[:], func=ACT.Silu)
+            nc.scalar.activation(out=active[:], in_=active[:], func=ACT.Copy, scale=gain_sb[:, g, t : t + 1])
+            return active
+
+        def add_held_turned(g, pair, actives, name):
+            turned = keep.tile([P, M // P, P, 2], BF16, name=name, align_bytes=64)
             for c in range(CHUNKS):
                 bank = psum.tile([P, 2, 2, P], F32, name="turn_bank", bufs=3)
-                for kk in range(2):
-                    cols = slice(c * CHUNK + kk * P, c * CHUNK + (kk + 1) * P)
+                for side in range(2):
+                    cols = slice(c * CHUNK + side * P, c * CHUNK + (side + 1) * P)
                     for e in range(2):
-                        nc.tensor.matmul(bank[:, kk, e, :], rows[e][:, cols], ident[:], start=True, stop=False, is_transpose=True)
-                        nc.tensor.matmul(bank[:, kk, e, :], held_sb[0][:, 2 * pair + e, cols], ident[:], start=False, stop=True, is_transpose=True)
+                        add_turned(bank[:, side, e, :], actives[e][:, cols], held_sb[g][:, 2 * pair + e, cols])
                 nc.scalar.copy(out=turned[:, 2 * c : 2 * c + 2], in_=bank[:].rearrange("m k e p -> m k p e"))
             return turned[:].rearrange("m k p e -> m (k p e)").bitcast(F32)
 
-        def turn_back(pairs, c):
+        def new_z_woven(g, c):
+            z_woven[g, c] = ring.tile([P, CHUNK * PACK], BF16, name="z_woven", bufs=CHUNKS, align_bytes=64)
+            return z_woven[g, c]
+
+        def weave_group0(pair_words, c):
             bank = psum.tile([P, 2, CHUNK], F32, name="turn_bank", bufs=3)
             for pair in range(2):
-                for kk in range(2):
-                    k = 2 * c + kk
-                    nc.tensor.transpose(bank[:, pair, kk * P : (kk + 1) * P], pairs[pair][:, k * P : (k + 1) * P], ident[:])
+                for side in range(2):
+                    k = 2 * c + side
+                    nc.tensor.transpose(bank[:, pair, side * P : (side + 1) * P], pair_words[pair][:, k * P : (k + 1) * P], ident[:])
             nc.scalar.copy(
-                out=new_woven(0, c)[:].bitcast(F32).rearrange("p (m u) -> p m u", u=2), in_=bank[:].rearrange("p u m -> p m u")
+                out=new_z_woven(0, c)[:].bitcast(F32).rearrange("p (m u) -> p m u", u=2), in_=bank[:].rearrange("p u m -> p m u")
             )
 
         def quantize_z(g, c):
-            cols = slice(g * M + c * CHUNK, g * M + (c + 1) * CHUNK)
-            nc.vector.quantize_mx(out=z_w[:, cols].bitcast(FP8X4), scales=z_s[:, cols], in_=z_woven[g, c][:])
+            quantize(z_w, z_s, slice(g * M + c * CHUNK, g * M + (c + 1) * CHUNK), z_woven[g, c])
 
         y_bank = {}
+        all_banks = [("b_bank", 2)] * 2 + [("ad_bank", 3)] * 3 + [("turn_bank", 3)] * 3
 
         def project(g, k):
             if g == 0:
-                tag, bufs = ([("b_bank", 2)] * 2 + [("ad_bank", 3)] * 3 + [("turn_bank", 3)] * 3)[k]
-                y_bank[k] = psum.tile([P, PACK, P], F32, name=tag, bufs=bufs)
+                y_bank[k] = psum.tile([P, PACK, P], F32, name=all_banks[k][0], bufs=all_banks[k][1])
             cols = slice(g * M + k * P, g * M + (k + 1) * P)
             for t in range(PACK):
-                rows = slice(g * N + t * P, g * N + (t + 1) * P)
+                outputs = slice(g * N + t * P, g * N + (t + 1) * P)
                 nc.tensor.matmul_mx(
-                    out=y_bank[k][:, t, :], lhsT=wo_w[:, rows].bitcast(FP8X4), lhsT_scale=wo_s[:, rows],
+                    out=y_bank[k][:, t, :], lhsT=wo_w[:, outputs].bitcast(FP8X4), lhsT_scale=wo_s[:, outputs],
                     rhs=z_w[:, cols].bitcast(FP8X4), rhs_scale=z_s[:, cols],
                     start=(g == 0 and t == 0), stop=(g == GROUPS - 1 and t == PACK - 1),
                 )
 
-        gather_table(0)
-        gather_table(1)
-        halves = []
-        for e in range(2):
-            halves.append(keep.tile([P, CHUNK * PACK], BF16, name=f"staged_then_page{e}", align_bytes=64))
-            round_w1(halves[e][:], raw_first[:, :, e * CHUNK : (e + 1) * CHUNK])
+        for half in range(2):
+            cols = slice(half * HALF, (half + 1) * HALF)
+            entries = list1[:, half * HALF // PER_COL : (half + 1) * HALF // PER_COL]
+            nc.vector.tensor_copy(v_w[:, cols], tab_w[:].indirect(entries))
+            nc.vector.tensor_copy(v_s[:, cols], tab_s[:].indirect(entries))
+        w1_woven0 = []
+        for half in range(2):
+            w1_woven0.append(keep.tile([P, GROUP // 2 * PACK], BF16, name=f"w1_then_page{2 + half}", align_bytes=64))
+            round_w1(w1_woven0[half][:], w1_raw0[:, :, half * GROUP // 2 : (half + 1) * GROUP // 2])
         for u in range(2):
-            front_bd(0, u)
-        w1_w = keep.tile([P, H], U32, name="tab_s_then_w1", align_bytes=64)
-        for e in range(2):
-            cols = slice(e * CHUNK, (e + 1) * CHUNK)
-            nc.vector.quantize_mx(out=w1_w[:, cols].bitcast(FP8X4), scales=w1_s[:, cols], in_=halves[e][:])
+            products_d_b(0, u)
+        w1_w = keep.tile([P, H], U32, name="tab_s_then_w1_then_active", align_bytes=64)
+        for half in range(2):
+            quantize(w1_w, w1_s, slice(half * GROUP // 2, (half + 1) * GROUP // 2), w1_woven0[half])
         for u in range(2):
-            front_a(0, u)
+            product_a(0, u)
             gate(0, u)
-        for e in range(2):
-            pages.append(keep.tile([P, T2], F32, name=f"staged_then_page{e}", align_bytes=64))
-            nc.vector.memset(pages[2 + e][:], 0.0)
-        after_tab = keep.tile([P, 2 * PACK * HALF + GROUPS * PACK], F32, name="tab_then_wg", align_bytes=64)
-        wg_late = keep.tile([P, PACK, HALF], F32, name="raw_then_wg")
+        for t in range(2, PACK):
+            pages.append(keep.tile([P, T2], F32, name=f"w1_then_page{t}", align_bytes=64))
+            nc.vector.memset(pages[t][:], 0.0)
+
+        after_tab = keep.tile([P, 2 * PACK * HALF + GROUPS * PACK], F32, name="tab_w_then_factors", align_bytes=64)
+        wg_late = keep.tile([P, PACK, HALF], F32, name="w1_raw0_then_wgs")
         wg = [after_tab[:, : PACK * HALF].rearrange("p (t j) -> p t j", t=PACK), wg_late[:]]
-        raw = after_tab[:, PACK * HALF : 2 * PACK * HALF].rearrange("p (i c) -> p i c", i=PACK)
+        weight_raw = after_tab[:, PACK * HALF : 2 * PACK * HALF].rearrange("p (i c) -> p i c", i=PACK)
         gain_sb = after_tab[:, 2 * PACK * HALF :].rearrange("p (g t) -> p g t", t=PACK)
-        load_wgs(wg[0][:, :, 0:CHUNK], 0, CHUNK)
-        load_wgs(wg[0][:, :, CHUNK:HALF], CHUNK, HALF)
-        load_raw(raw, w1[:, GROUP : 2 * GROUP])
+        load_wgs(wg[0][:, :, 0:QUARTER], 0, QUARTER)
+        load_wgs(wg[0][:, :, QUARTER:HALF], QUARTER, HALF)
+        load_weight(weight_raw, w1[:, GROUP : 2 * GROUP])
         nc.sync.dma_start(out=gain_sb, in_=gain.rearrange("(g p t) -> p g t", p=P, t=PACK))
         load_wgs(wg[1], HALF, S)
 
-        back(0, 0, 0)
-        rows = []
         rounds = [(g, quarter) for g in range(GROUPS) for quarter in range(QUARTERS)]
 
-        def fronts(r):
-            g, quarter = rounds[r]
+        def products(g, quarter):
             for u in (2 * quarter, 2 * quarter + 1):
-                front_bd(g, u)
+                products_d_b(g, u)
                 gate(g, u)
-                front_a(g, u)
+                product_a(g, u)
 
-        for r, (g, quarter) in enumerate(rounds):
-            if r == 0:
-                back(g, quarter, 1)
-                fronts(1)
-            if 0 == 0 and r + 2 < len(rounds):
-                fronts(r + 2)
-            if r + 1 < len(rounds):
-                back(*rounds[r + 1], 0)
-                back(*rounds[r + 1], 1)
-            if 0 == 1 and r + 2 < len(rounds):
-                fronts(r + 2)
-            for t in range(PACK):
-                scatter(g, t, quarter * CHUNK, (quarter + 1) * CHUNK)
-                if (g, quarter) == (0, QUARTERS - 1):
-                    rows.append(fetch_rows(t))
-            if r == 0:
-                staged = keep.tile([P, GROUP * PACK], BF16, name="then_held0", align_bytes=64)
-                for c in range(4):
-                    round_w1(staged[:, c * GROUP : (c + 1) * GROUP], raw[:, :, c * P : (c + 1) * P])
-                quantize(w1_w, w1_s, 1, staged)
-                held_sb[0] = load_held(0, "then_held0")
-                load_raw(raw, wo[0:GROUP, :])
-        held_sb[1] = load_held(1, "w2_s")
-        codes = keep.tile([P, GROUPS * (N + M)], U32, name="wide1", align_bytes=64)
-        wo_w, z_w = codes[:, : GROUPS * N], codes[:, GROUPS * N :]
-        pairs = []
         for pair in range(2):
-            active = []
-            for t in (2 * pair, 2 * pair + 1):
-                active.append(keep.tile([P, M], F32, name=("v_w", "w3_w", "tab_s_then_w1", "w2_w")[t], align_bytes=64))
-                nc.scalar.activation(out=active[-1][:], in_=rows[t][:], func=ACT.Silu)
-                nc.scalar.activation(out=active[-1][:], in_=active[-1][:], func=ACT.Copy, scale=gain_sb[:, 0, t : t + 1])
-            pairs.append(add_held_turned(pair, active))
-            quantize(wo_w, wo_s, pair, round_wo(pair, raw))
+            make_h(0, 0, pair)
+        products(*rounds[1])
+        x_group0 = []
+        for r, (g, quarter) in enumerate(rounds[:-1]):
+            if r + 2 < len(rounds):
+                products(*rounds[r + 2])
+            for pair in range(2):
+                make_h(*rounds[r + 1], pair)
+            if g == 0:
+                for t in range(PACK):
+                    scatter(pages[t], 0, t, quarter * QUARTER, (quarter + 1) * QUARTER)
+                    if quarter == QUARTERS - 1:
+                        x_group0.append(fetch_slot(t))
+            if r == 0:
+                w1_woven1 = keep.tile([P, GROUP * PACK], BF16, name="gated_then_w1_then_held0", align_bytes=64)
+                for piece in range(PACK):
+                    round_w1(w1_woven1[:, piece * GROUP : (piece + 1) * GROUP], weight_raw[:, :, piece * P : (piece + 1) * P])
+                quantize(w1_w, w1_s, slice(GROUP, 2 * GROUP), w1_woven1)
+                held_sb[0] = load_held(0, "gated_then_w1_then_held0")
+                load_weight(weight_raw, wo[0:GROUP, :])
+        held_sb[1] = load_held(1, "w2_s_then_held1")
+
+        for t in range(2):
+            for half in range(2):
+                scatter(pages[t], 1, t, half * HALF, (half + 1) * HALF)
+        active_names = ("v_w_then_active", "w3_w_then_active", "tab_s_then_w1_then_active", "w2_w_then_active")
+        pair_names = ("turned0_then_active", "turned1_then_active_then_x")
+        wo_woven, pair_words = [], []
+        for pair in range(2):
+            actives = [activate(x_group0[t], 0, t, active_names[t]) for t in (2 * pair, 2 * pair + 1)]
+            pair_words.append(add_held_turned(0, pair, actives, pair_names[pair]))
+            wo_woven.append(round_wo(weight_raw, ("w3_s_then_wo0", "w1_s_then_wo1")[pair]))
             if pair == 0:
-                load_raw(raw, wo[GROUP : 2 * GROUP, :])
+                load_weight(weight_raw, wo[GROUP : 2 * GROUP, :])
         for c in range(CHUNKS):
-            turn_back(pairs, c)
+            weave_group0(pair_words, c)
+
+        actives = [activate(fetch_slot(t), 1, t, pair_names[t]) for t in range(2)]
+        for t in range(2, PACK):
+            for half in range(2):
+                scatter(pages[t - 2], 1, t, half * HALF, (half + 1) * HALF)
+        early_words = add_held_turned(1, 0, actives, "x2_then_turned_then_wo_s")
+        z_slots = keep.tile([P, PACK, M], BF16, name="z_slots")
+        for half in range(2):
+            bank = psum.tile([P, HALF], F32, name="turn_bank", bufs=3)
+            for side in range(HALF // P):
+                k = half * (HALF // P) + side
+                nc.tensor.transpose(bank[:, side * P : (side + 1) * P], early_words[:, k * P : (k + 1) * P], ident[:])
+            nc.scalar.copy(
+                out=z_slots[:, 0:2, half * HALF : (half + 1) * HALF], in_=bank[:].bitcast(BF16).rearrange("p (m e) -> p e m", e=2)
+            )
+
+        codes = keep.tile([P, GROUPS * (N + M)], U32, name="h1_then_codes", align_bytes=64)
+        wo_s = keep.tile([P, GROUPS * N], U8, name="x2_then_turned_then_wo_s", align_bytes=64)
+        wo_w, z_w = codes[:, : GROUPS * N], codes[:, GROUPS * N :]
+        for c in range(CHUNKS):
             quantize_z(0, c)
+        for g in range(GROUPS):
+            quantize(wo_w, wo_s, slice(g * N, (g + 1) * N), wo_woven[g])
         for k in range(M // P):
             project(0, k)
 
-        y_sb = keep.tile([P, PACK, M], F32, name="wide0", align_bytes=64)
-        y_woven = {}
-        x_cols, z_cols = {}, {}
+        x_ring = keep.tile([P, 2, 2, CHUNK], F32, name="turned1_then_active_then_x", align_bytes=64)
+        y_sb = keep.tile([P, PACK, M], F32, name="h0_then_y", align_bytes=64)
 
-        def empty_y(c):
-            y_woven[c] = ring.tile([P, CHUNK * PACK], BF16, name="y_woven", bufs=3, align_bytes=64)
-            for e in range(CHUNK // P):
-                k = c * (CHUNK // P) + e
-                project(1, k)
-                nc.scalar.copy(out=y_sb[:, :, k * P : (k + 1) * P], in_=y_bank[k][:])
-            cols = slice(c * CHUNK, (c + 1) * CHUNK)
-            nc.sync.dma_start(out=out_0.rearrange("(p t) m -> p t m", t=PACK)[:, :, cols], in_=y_sb[:, :, cols])
-
-        def weave_y(c):
-            if c in YS:
-                for e in range(CHUNK // P):
-                    nc.scalar.copy(
-                        out=y_woven[c][:, e * GROUP : (e + 1) * GROUP].rearrange("p (m t) -> p m t", t=PACK),
-                        in_=y_bank[c * (CHUNK // P) + e][:].rearrange("p t m -> p m t"),
-                    )
-            else:
-                nc.vector.tensor_copy(
-                    out=y_woven[c][:].rearrange("p (m e t) -> p m t e", e=4, t=PACK),
-                    in_=y_sb[:, :, c * CHUNK : (c + 1) * CHUNK].rearrange("p t (m e) -> p m t e", e=4),
-                )
-
-        def quantize_y(c):
-            cols = slice(c * CHUNK, (c + 1) * CHUNK)
-            nc.vector.quantize_mx(out=y_w[:, cols].bitcast(FP8X4), scales=y_s[:, cols], in_=y_woven[c][:])
-            nc.sync.dma_start(out=out_1[0].rearrange("p m t -> p (m t)").bitcast(I32)[:, cols], in_=y_w[:, cols].bitcast(I32))
-
-        def fetch_cols(c):
-            x_cols[c] = keep.tile([P, PACK, CHUNK], F32, name=f"turned{c % 2}")
-            for t in range(PACK):
-                nc.vector.tensor_copy(x_cols[c][:, t, :], pages[t][:].indirect(list3[:, c * CHUNK // PER_COL : (c + 1) * CHUNK // PER_COL]))
-            nc.scalar.activation(out=x_cols[c][:], in_=x_cols[c][:], func=ACT.Silu)
-
-        def make_z(c):
-            z_cols[c] = ring.tile([P, PACK, CHUNK], BF16, name="z_cols")
-            for t in range(PACK):
-                nc.vector.scalar_tensor_tensor(
-                    out=z_cols[c][:, t, :], in0=x_cols[c][:, t, :], scalar=gain_sb[:, 1, t : t + 1],
-                    in1=held_sb[1][:, t, c * CHUNK : (c + 1) * CHUNK], op0=MULT, op1=ADD,
-                )
-            (nc.scalar.copy if c in ZS else nc.vector.tensor_copy)(
-                out=new_woven(1, c)[:].rearrange("p (m e t) -> p m t e", e=4, t=PACK),
-                in_=z_cols[c][:].rearrange("p t (m e) -> p m t e", e=4),
+        def weave(copy, woven, slots):
+            copy(
+                out=woven[:].rearrange("p (m e t) -> p m t e", e=NEIGHBOURS, t=PACK),
+                in_=slots.rearrange("p t (m e) -> p m t e", e=NEIGHBOURS),
             )
 
-        fetch_cols(0)
-        fetch_cols(1)
+        def fetch_chunk(c):
+            entries = list3[:, c * CHUNK // PER_COL : (c + 1) * CHUNK // PER_COL]
+            for e in range(2):
+                nc.vector.tensor_copy(x_ring[:, c % 2, e, :], pages[e][:].indirect(entries))
+            nc.scalar.activation(out=x_ring[:, c % 2], in_=x_ring[:, c % 2], func=ACT.Silu)
+
+        def make_z_chunk(c):
+            cols = slice(c * CHUNK, (c + 1) * CHUNK)
+            for e in range(2):
+                t = 2 + e
+                nc.vector.scalar_tensor_tensor(
+                    out=z_slots[:, t, cols], in0=x_ring[:, c % 2, e, :], scalar=gain_sb[:, 1, t : t + 1],
+                    in1=held_sb[1][:, t, cols], op0=MULT, op1=ADD,
+                )
+            weave(nc.scalar.copy if c < SCALAR_WEAVES else nc.vector.tensor_copy, new_z_woven(1, c), z_slots[:, :, cols])
+
+        def make_y_chunk(c):
+            cols = slice(c * CHUNK, (c + 1) * CHUNK)
+            for k in range(c * CHUNK // P, (c + 1) * CHUNK // P):
+                project(1, k)
+                nc.scalar.copy(out=y_sb[:, :, k * P : (k + 1) * P], in_=y_bank[k][:])
+            nc.sync.dma_start(out=out_0.rearrange("(p t) m -> p t m", t=PACK)[:, :, cols], in_=y_sb[:, :, cols])
+
+        def store_y_codes(c):
+            cols = slice(c * CHUNK, (c + 1) * CHUNK)
+            y_woven = ring.tile([P, CHUNK * PACK], BF16, name="y_woven", bufs=3, align_bytes=64)
+            weave(nc.vector.tensor_copy, y_woven, y_sb[:, :, cols])
+            quantize(y_w, y_s, cols, y_woven)
+            nc.sync.dma_start(out=out_1[0].rearrange("p m t -> p (m t)").bitcast(I32)[:, cols], in_=y_w[:, cols].bitcast(I32))
+
+        fetch_chunk(0)
+        fetch_chunk(1)
         for c in range(CHUNKS):
-            make_z(c)
+            make_z_chunk(c)
             if c + 2 < CHUNKS:
-                fetch_cols(c + 2)
+                fetch_chunk(c + 2)
             quantize_z(1, c)
-            if c >= LAG:
-                quantize_y(c - LAG)
-            empty_y(c)
-            weave_y(c)
-        for c in range(CHUNKS - LAG, CHUNKS):
-            quantize_y(c)
-        for q in range(4):
+            make_y_chunk(c)
+        for c in range(CHUNKS):
+            store_y_codes(c)
+        for q in range(QUADRANTS):
             nc.sync.dma_start(out=out_2[0, 4 * q : 4 * q + 4, :].bitcast(I32), in_=y_s[32 * q : 32 * q + 4, :].bitcast(I32))

from contextlib import ExitStack

import concourse.mybir as mybir
from concourse.masks import make_identity

K, H, N, T, S, T2, M = 512, 1024, 512, 4096, 1024, 2048, 1024
FLOPS = 2 * (3 * K * H * S + H * N * M)

F32 = mybir.dt.float32
BF16 = mybir.dt.bfloat16
I32 = mybir.dt.int32
U32 = mybir.dt.uint32
U16 = mybir.dt.uint16
U8 = mybir.dt.uint8
FP8X4 = mybir.dt.float8_e4m3fn_x4
FP4X4 = mybir.dt.float4_e2m1fn_x4
MULT = mybir.AluOpType.mult
ADD = mybir.AluOpType.add
ACT = mybir.ActivationFunctionType

P = 128
PACK = 4
GROUP = P * PACK
GROUPS = H // GROUP
QUADRANTS = 4
PER_COL = 16
HALF = S // 2
QUARTER = S // 4
QUARTERS = S // QUARTER
CHUNK = 256
CHUNKS = M // CHUNK
NEIGHBOURS = 4
VECTOR_UNITS = 2
SCALAR_WEAVES = 2


def tile_list_reshard_resume_features_kernel(
    tc, tab_words, tab_scales, offs, w1, w2_words, w2_scales, w3_words, w3_scales,
    wgs, offs2, offs3, gain, held, wo, out_0, out_1, out_2,
):
    nc = tc.nc
    with ExitStack() as ctx:
        keep = ctx.enter_context(tc.tile_pool(name="keep", bufs=1))
        ring = ctx.enter_context(tc.tile_pool(name="ring", bufs=2))
        psum = ctx.enter_context(tc.psum_pool(name="psum", bufs=1))

        list1 = keep.tile([P, S // PER_COL], U16, name="list1")
        list2 = keep.tile([P, S // PER_COL], U16, name="list2")
        list3 = keep.tile([P, M // PER_COL], U16, name="list3")
        tab_w = keep.tile([P, T], U32, name="tab_w_then_factors", align_bytes=64)
        tab_s = keep.tile([P, T], U8, name="tab_s_then_w1_then_active", align_bytes=64)
        v_w = keep.tile([P, S], U32, name="v_w_then_active", align_bytes=64)
        v_s = keep.tile([P, S], U8, name="v_s", align_bytes=64)
        w1_s = keep.tile([P, H], U8, name="w1_s_then_wo1", align_bytes=64)
        w2_w = keep.tile([P, 2 * H], U8, name="w2_w_then_active", align_bytes=64)
        w2_s = keep.tile([P, H], U8, name="w2_s_then_held1", align_bytes=64)
        w3_w = keep.tile([P, H], U32, name="w3_w_then_active", align_bytes=64)
        w3_s = keep.tile([P, H], U8, name="w3_s_then_wo0", align_bytes=64)
        z_s = keep.tile([P, GROUPS * M], U8, name="z_s", align_bytes=64)
        y_w = keep.tile([P, M], U32, name="y_w", align_bytes=64)
        y_s = keep.tile([P, M], U8, name="y_s", align_bytes=64)
        ident = keep.tile([P, P], F32, name="ident")
        pages = [keep.tile([P, T2], F32, name=f"page{t}") for t in range(2)]

        def load_scales(queue, plane, scales, quadrants):
            for q in quadrants:
                queue.dma_start(out=plane[32 * q : 32 * q + 4, :].bitcast(I32), in_=scales[0, 4 * q : 4 * q + 4, :].bitcast(I32))

        def load_weight(raw, weight):
            nc.sync.dma_start(out=raw, in_=weight.rearrange("(p i) c -> p i c", i=PACK))

        def load_wgs(part, lo, hi):
            for q in (0, 2, 1, 3):
                nc.sync.dma_start(out=part[32 * q : 32 * q + 32], in_=wgs.rearrange("(p t) j -> p t j", t=PACK)[:, :, lo:hi])

        def load_held(g, name):
            dealt_held = keep.tile([P, PACK, M], F32, name=name, align_bytes=64)
            nc.sync.dma_start(out=dealt_held[:], in_=held[g * GROUP : (g + 1) * GROUP, :].rearrange("(p t) m -> p t m", t=PACK))
            return dealt_held

        nc.sync.dma_start(list1[:], offs)
        nc.sync.dma_start(list2[:], offs2)
        nc.sync.dma_start(list3[:], offs3)
        nc.sync.dma_start(out=tab_w[:].bitcast(I32), in_=tab_words[0].rearrange("p t i -> p (t i)").bitcast(I32))
        w1_raw0 = keep.tile([P, PACK, GROUP], F32, name="w1_raw0_then_wgs")
        load_weight(w1_raw0[:], w1[:, 0:GROUP])
        nc.sync.dma_start(out=w3_w[:].bitcast(I32), in_=w3_words[0].rearrange("p c i -> p (c i)").bitcast(I32))
        nc.sync.dma_start(out=w2_w[:].bitcast(I32), in_=w2_words[0].bitcast(I32))
        nc.vector.memset(tab_s[:].bitcast(I32), 0)
        load_scales(nc.scalar, tab_s, tab_scales, range(QUADRANTS))
        nc.gpsimd.memset(w3_s[:].bitcast(I32), 0)
        load_scales(nc.gpsimd, w3_s, w3_scales, range(QUADRANTS))
        nc.vector.memset(w2_s[:].bitcast(I32), 0)
        load_scales(nc.gpsimd, w2_s, w2_scales, range(QUADRANTS - 1))
        load_scales(nc.scalar, w2_s, w2_scales, [QUADRANTS - 1])
        make_identity(nc, ident[:])
        for page in pages:
            nc.vector.memset(page[:, : T2 // 2 - 1], 0.0)
            nc.vector.memset(page[:, T2 // 2 - 1 :], 0.0)

        def round_w1(woven, raw):
            nc.scalar.copy(
                out=woven.rearrange("p (c e i) -> p c i e", e=NEIGHBOURS, i=PACK),
                in_=raw.rearrange("p i (c e) -> p c i e", e=NEIGHBOURS),
            )

        def round_wo(raw, name):
            woven = keep.tile([P, GROUP * PACK], BF16, name=name, align_bytes=64)
            width = P // PACK
            for piece in range(PACK):
                cols = slice(piece * width, (piece + 1) * width)
                nc.scalar.copy(
                    out=woven[:].rearrange("p (t c i) -> p c t i", t=PACK, i=PACK)[:, cols],
                    in_=raw.rearrange("p i (c t) -> p c t i", t=PACK)[:, cols],
                )
            return woven

        def quantize(words, scales, cols, woven):
            nc.vector.quantize_mx(out=words[:, cols].bitcast(FP8X4), scales=scales[:, cols], in_=woven[:])

        b_bank, b_sb, tanh_d, a_sb, gated, h_sb = {}, {}, {}, {}, {}, {}

        def dealt(bank):
            return bank[:].rearrange("j (p t) -> j t p", t=PACK)

        def product(bank, u, moving, moving_scales):
            tokens = slice(u * P, (u + 1) * P)
            nc.tensor.matmul_mx(
                out=bank[:], lhsT=v_w[:, tokens].bitcast(FP8X4), lhsT_scale=v_s[:, tokens],
                rhs=moving, rhs_scale=moving_scales, start=True, stop=True,
            )

        def on_vector(g, u):
            return g == 0 and u < VECTOR_UNITS

        def products_d_b(g, u):
            cols = slice(g * GROUP, (g + 1) * GROUP)
            d_bank = psum.tile([P, GROUP], F32, name="ad_bank", bufs=3)
            product(d_bank, u, w3_w[:, cols].bitcast(FP8X4), w3_s[:, cols])
            b_bank[g, u] = psum.tile([P, GROUP], F32, name="b_bank", bufs=2)
            product(b_bank[g, u], u, w2_w[:, 2 * g * GROUP : 2 * (g + 1) * GROUP].bitcast(FP4X4), w2_s[:, cols])
            tanh_d[g, u] = ring.tile([P, PACK, P], F32, name="tanh_d")
            nc.scalar.activation(out=tanh_d[g, u][:], in_=dealt(d_bank), func=ACT.Tanh)
            if not on_vector(g, u):
                b_sb[g, u] = ring.tile([P, PACK, P], F32, name="b_sb")
                nc.scalar.copy(out=b_sb[g, u][:], in_=dealt(b_bank[g, u]))

        def product_a(g, u):
            cols = slice(g * GROUP, (g + 1) * GROUP)
            a_bank = psum.tile([P, GROUP], F32, name="ad_bank", bufs=3)
            product(a_bank, u, w1_w[:, cols].bitcast(FP8X4), w1_s[:, cols])
            a_sb[g, u] = ring.tile([P, PACK, P], F32, name="a_sb", bufs=4)
            nc.scalar.copy(out=a_sb[g, u][:], in_=dealt(a_bank))

        def gate(g, u):
            if (g, u) == (0, 1):
                gated[g, u] = keep.tile([P, PACK, P], F32, name="gated_then_w1_then_held0", align_bytes=64)
            else:
                gated[g, u] = ring.tile([P, PACK, P], F32, name="gated", bufs=4)
            if on_vector(g, u):
                nc.vector.tensor_tensor(gated[g, u][:], dealt(b_bank[g, u]), tanh_d[g, u][:], MULT)
            else:
                nc.gpsimd.tensor_tensor(gated[g, u][:], b_sb[g, u][:], tanh_d[g, u][:], MULT)

        def add_turned(out, first, second):
            nc.tensor.matmul(out, first, ident[:], start=True, stop=False, is_transpose=True)
            nc.tensor.matmul(out, second, ident[:], start=False, stop=True, is_transpose=True)

        def factors(slots, lo, hi):
            return wg[lo // HALF][:, slots, lo % HALF : lo % HALF + hi - lo]

        def make_h(g, quarter, pair):
            if (quarter, pair) == (0, 0):
                h_sb[g] = keep.tile([P, PACK, S], F32, name=("h0_then_y", "h1_then_codes")[g], align_bytes=64)
            h_bank = psum.tile([P, 2, QUARTER], F32, name="turn_bank", bufs=3)
            for e in range(2):
                for side in range(2):
                    u, t = 2 * quarter + side, 2 * pair + e
                    add_turned(h_bank[:, e, side * P : (side + 1) * P], a_sb[g, u][:, t, :], gated[g, u][:, t, :])
            slots, lo, hi = slice(2 * pair, 2 * pair + 2), quarter * QUARTER, (quarter + 1) * QUARTER
            nc.scalar.copy(out=h_sb[g][:, slots, lo:hi], in_=h_bank[:])
            if g == 0:
                nc.gpsimd.tensor_tensor(h_sb[g][:, slots, lo:hi], h_sb[g][:, slots, lo:hi], factors(slots, lo, hi), MULT)

        def scatter(page, g, t, lo, hi):
            window = page[:].indirect(list2[:, lo // PER_COL : hi // PER_COL])
            if g == 0:
                nc.vector.tensor_copy(window, h_sb[g][:, t, lo:hi])
            else:
                nc.vector.tensor_tensor(window, h_sb[g][:, t, lo:hi], factors(t, lo, hi), MULT)

        def fetch_slot(t):
            x = keep.tile([P, M], F32, name=("x0", "x1", "x2_then_turned_then_wo_s", "x3")[t], align_bytes=64)
            nc.vector.tensor_copy(x[:], pages[t][:].indirect(list3[:]))
            return x

        held_sb, z_woven = {}, {}

        def activate(x, g, t, name):
            active = keep.tile([P, M], F32, name=name, align_bytes=64)
            nc.scalar.activation(out=active[:], in_=x[:], func=ACT.Silu)
            nc.scalar.activation(out=active[:], in_=active[:], func=ACT.Copy, scale=gain_sb[:, g, t : t + 1])
            return active

        def add_held_turned(g, pair, actives, name):
            turned = keep.tile([P, M // P, P, 2], BF16, name=name, align_bytes=64)
            for c in range(CHUNKS):
                bank = psum.tile([P, 2, 2, P], F32, name="turn_bank", bufs=3)
                for side in range(2):
                    cols = slice(c * CHUNK + side * P, c * CHUNK + (side + 1) * P)
                    for e in range(2):
                        add_turned(bank[:, side, e, :], actives[e][:, cols], held_sb[g][:, 2 * pair + e, cols])
                nc.scalar.copy(out=turned[:, 2 * c : 2 * c + 2], in_=bank[:].rearrange("m k e p -> m k p e"))
            return turned[:].rearrange("m k p e -> m (k p e)").bitcast(F32)

        def new_z_woven(g, c):
            z_woven[g, c] = ring.tile([P, CHUNK * PACK], BF16, name="z_woven", bufs=CHUNKS, align_bytes=64)
            return z_woven[g, c]

        def weave_group0(pair_words, c):
            bank = psum.tile([P, 2, CHUNK], F32, name="turn_bank", bufs=3)
            for pair in range(2):
                for side in range(2):
                    k = 2 * c + side
                    nc.tensor.transpose(bank[:, pair, side * P : (side + 1) * P], pair_words[pair][:, k * P : (k + 1) * P], ident[:])
            nc.scalar.copy(
                out=new_z_woven(0, c)[:].bitcast(F32).rearrange("p (m u) -> p m u", u=2), in_=bank[:].rearrange("p u m -> p m u")
            )

        def quantize_z(g, c):
            quantize(z_w, z_s, slice(g * M + c * CHUNK, g * M + (c + 1) * CHUNK), z_woven[g, c])

        y_bank = {}
        all_banks = [("b_bank", 2)] * 2 + [("ad_bank", 3)] * 3 + [("turn_bank", 3)] * 3

        def project(g, k):
            if g == 0:
                y_bank[k] = psum.tile([P, PACK, P], F32, name=all_banks[k][0], bufs=all_banks[k][1])
            cols = slice(g * M + k * P, g * M + (k + 1) * P)
            for t in range(PACK):
                outputs = slice(g * N + t * P, g * N + (t + 1) * P)
                nc.tensor.matmul_mx(
                    out=y_bank[k][:, t, :], lhsT=wo_w[:, outputs].bitcast(FP8X4), lhsT_scale=wo_s[:, outputs],
                    rhs=z_w[:, cols].bitcast(FP8X4), rhs_scale=z_s[:, cols],
                    start=(g == 0 and t == 0), stop=(g == GROUPS - 1 and t == PACK - 1),
                )

        for half in range(2):
            cols = slice(half * HALF, (half + 1) * HALF)
            entries = list1[:, half * HALF // PER_COL : (half + 1) * HALF // PER_COL]
            nc.vector.tensor_copy(v_w[:, cols], tab_w[:].indirect(entries))
            nc.vector.tensor_copy(v_s[:, cols], tab_s[:].indirect(entries))
        w1_woven0 = []
        for half in range(2):
            w1_woven0.append(keep.tile([P, GROUP // 2 * PACK], BF16, name=f"w1_then_page{2 + half}", align_bytes=64))
            round_w1(w1_woven0[half][:], w1_raw0[:, :, half * GROUP // 2 : (half + 1) * GROUP // 2])
        for u in range(2):
            products_d_b(0, u)
        w1_w = keep.tile([P, H], U32, name="tab_s_then_w1_then_active", align_bytes=64)
        for half in range(2):
            quantize(w1_w, w1_s, slice(half * GROUP // 2, (half + 1) * GROUP // 2), w1_woven0[half])
        for u in range(2):
            product_a(0, u)
            gate(0, u)
        for t in range(2, PACK):
            pages.append(keep.tile([P, T2], F32, name=f"w1_then_page{t}", align_bytes=64))
            nc.vector.memset(pages[t][:], 0.0)

        after_tab = keep.tile([P, 2 * PACK * HALF + GROUPS * PACK], F32, name="tab_w_then_factors", align_bytes=64)
        wg_late = keep.tile([P, PACK, HALF], F32, name="w1_raw0_then_wgs")
        wg = [after_tab[:, : PACK * HALF].rearrange("p (t j) -> p t j", t=PACK), wg_late[:]]
        weight_raw = after_tab[:, PACK * HALF : 2 * PACK * HALF].rearrange("p (i c) -> p i c", i=PACK)
        gain_sb = after_tab[:, 2 * PACK * HALF :].rearrange("p (g t) -> p g t", t=PACK)
        load_wgs(wg[0][:, :, 0:QUARTER], 0, QUARTER)
        load_wgs(wg[0][:, :, QUARTER:HALF], QUARTER, HALF)
        load_weight(weight_raw, w1[:, GROUP : 2 * GROUP])
        nc.sync.dma_start(out=gain_sb, in_=gain.rearrange("(g p t) -> p g t", p=P, t=PACK))
        load_wgs(wg[1], HALF, S)

        rounds = [(g, quarter) for g in range(GROUPS) for quarter in range(QUARTERS)]

        def products(g, quarter):
            for u in (2 * quarter, 2 * quarter + 1):
                products_d_b(g, u)
                gate(g, u)
                product_a(g, u)

        for pair in range(2):
            make_h(0, 0, pair)
        products(*rounds[1])
        x_group0 = []
        for r, (g, quarter) in enumerate(rounds[:-1]):
            if r + 2 < len(rounds):
                products(*rounds[r + 2])
            for pair in range(2):
                make_h(*rounds[r + 1], pair)
            if g == 0:
                for t in range(PACK):
                    scatter(pages[t], 0, t, quarter * QUARTER, (quarter + 1) * QUARTER)
                    if quarter == QUARTERS - 1:
                        x_group0.append(fetch_slot(t))
            if r == 0:
                w1_woven1 = keep.tile([P, GROUP * PACK], BF16, name="gated_then_w1_then_held0", align_bytes=64)
                for piece in range(PACK):
                    round_w1(w1_woven1[:, piece * GROUP : (piece + 1) * GROUP], weight_raw[:, :, piece * P : (piece + 1) * P])
                quantize(w1_w, w1_s, slice(GROUP, 2 * GROUP), w1_woven1)
                held_sb[0] = load_held(0, "gated_then_w1_then_held0")
                load_weight(weight_raw, wo[0:GROUP, :])
        held_sb[1] = load_held(1, "w2_s_then_held1")

        for t in range(2):
            for half in range(2):
                scatter(pages[t], 1, t, half * HALF, (half + 1) * HALF)
        active_names = ("v_w_then_active", "w3_w_then_active", "tab_s_then_w1_then_active", "w2_w_then_active")
        pair_names = ("turned0_then_active", "turned1_then_active_then_x")
        wo_woven, pair_words = [], []
        for pair in range(2):
            actives = [activate(x_group0[t], 0, t, active_names[t]) for t in (2 * pair, 2 * pair + 1)]
            pair_words.append(add_held_turned(0, pair, actives, pair_names[pair]))
            wo_woven.append(round_wo(weight_raw, ("w3_s_then_wo0", "w1_s_then_wo1")[pair]))
            if pair == 0:
                load_weight(weight_raw, wo[GROUP : 2 * GROUP, :])
        for c in range(CHUNKS):
            weave_group0(pair_words, c)

        actives = [activate(fetch_slot(t), 1, t, pair_names[t]) for t in range(2)]
        for t in range(2, PACK):
            for half in range(2):
                scatter(pages[t - 2], 1, t, half * HALF, (half + 1) * HALF)
        early_words = add_held_turned(1, 0, actives, "x2_then_turned_then_wo_s")
        z_slots = keep.tile([P, PACK, M], BF16, name="z_slots")
        for half in range(2):
            bank = psum.tile([P, HALF], F32, name="turn_bank", bufs=3)
            for side in range(HALF // P):
                k = half * (HALF // P) + side
                nc.tensor.transpose(bank[:, side * P : (side + 1) * P], early_words[:, k * P : (k + 1) * P], ident[:])
            nc.scalar.copy(
                out=z_slots[:, 0:2, half * HALF : (half + 1) * HALF], in_=bank[:].bitcast(BF16).rearrange("p (m e) -> p e m", e=2)
            )

        codes = keep.tile([P, GROUPS * (N + M)], U32, name="h1_then_codes", align_bytes=64)
        wo_s = keep.tile([P, GROUPS * N], U8, name="x2_then_turned_then_wo_s", align_bytes=64)
        wo_w, z_w = codes[:, : GROUPS * N], codes[:, GROUPS * N :]
        for c in range(CHUNKS):
            quantize_z(0, c)
        for g in range(GROUPS):
            quantize(wo_w, wo_s, slice(g * N, (g + 1) * N), wo_woven[g])
        for k in range(M // P):
            project(0, k)

        x_ring = keep.tile([P, 2, 2, CHUNK], F32, name="turned1_then_active_then_x", align_bytes=64)
        y_sb = keep.tile([P, PACK, M], F32, name="h0_then_y", align_bytes=64)

        def weave(copy, woven, slots):
            copy(
                out=woven[:].rearrange("p (m e t) -> p m t e", e=NEIGHBOURS, t=PACK),
                in_=slots.rearrange("p t (m e) -> p m t e", e=NEIGHBOURS),
            )

        def fetch_chunk(c):
            entries = list3[:, c * CHUNK // PER_COL : (c + 1) * CHUNK // PER_COL]
            for e in range(2):
                nc.vector.tensor_copy(x_ring[:, c % 2, e, :], pages[e][:].indirect(entries))
            nc.scalar.activation(out=x_ring[:, c % 2], in_=x_ring[:, c % 2], func=ACT.Silu)

        def make_z_chunk(c):
            cols = slice(c * CHUNK, (c + 1) * CHUNK)
            for e in range(2):
                t = 2 + e
                nc.vector.scalar_tensor_tensor(
                    out=z_slots[:, t, cols], in0=x_ring[:, c % 2, e, :], scalar=gain_sb[:, 1, t : t + 1],
                    in1=held_sb[1][:, t, cols], op0=MULT, op1=ADD,
                )
            weave(nc.scalar.copy if c < SCALAR_WEAVES else nc.vector.tensor_copy, new_z_woven(1, c), z_slots[:, :, cols])

        def make_y_chunk(c):
            cols = slice(c * CHUNK, (c + 1) * CHUNK)
            for k in range(c * CHUNK // P, (c + 1) * CHUNK // P):
                project(1, k)
                nc.scalar.copy(out=y_sb[:, :, k * P : (k + 1) * P], in_=y_bank[k][:])
            nc.sync.dma_start(out=out_0.rearrange("(p t) m -> p t m", t=PACK)[:, :, cols], in_=y_sb[:, :, cols])

        def store_y_codes(c):
            cols = slice(c * CHUNK, (c + 1) * CHUNK)
            y_woven = ring.tile([P, CHUNK * PACK], BF16, name="y_woven", bufs=3, align_bytes=64)
            weave(nc.vector.tensor_copy, y_woven, y_sb[:, :, cols])
            quantize(y_w, y_s, cols, y_woven)
            nc.sync.dma_start(out=out_1[0].rearrange("p m t -> p (m t)").bitcast(I32)[:, cols], in_=y_w[:, cols].bitcast(I32))

        fetch_chunk(0)
        fetch_chunk(1)
        for c in range(CHUNKS):
            make_z_chunk(c)
            if c + 2 < CHUNKS:
                fetch_chunk(c + 2)
            quantize_z(1, c)
            make_y_chunk(c)
        for c in range(CHUNKS):
            store_y_codes(c)
        for q in range(QUADRANTS):
            nc.sync.dma_start(out=out_2[0, 4 * q : 4 * q + 4, :].bitcast(I32), in_=y_s[32 * q : 32 * q + 4, :].bitcast(I32))
